import numpy as np
import ml_dtypes


def mxq(x, axis, fmt="e4m3"):
    dtype, down = {"e4m3": (ml_dtypes.float8_e4m3fn, 7), "e5m2": (ml_dtypes.float8_e5m2, 14)}[fmt]
    v = np.moveaxis(np.asarray(x, np.float32).astype(ml_dtypes.bfloat16).astype(np.float64), axis, -1)
    blocks = v.reshape(v.shape[:-1] + (-1, 32))
    amax = np.abs(blocks).max(-1, keepdims=True)
    byte = np.maximum(np.where(amax > 0, np.frexp(amax)[1] - 1 + 127, 0) - down, 1)
    scale = np.exp2(byte - 127.0)
    codes = (blocks / scale).astype(np.float32).astype(dtype).astype(np.float64)
    return np.moveaxis((codes * scale).reshape(v.shape), -1, axis)


WIDE = False


def mx_kscale(k):
    if not WIDE:
        return np.ones(k)
    levels = np.array([10, -10, 5, -5, 0])
    if k % 512:
        return np.exp2(np.random.permutation(np.resize(levels, k // 32))).repeat(32)
    a = np.empty((k // 512, 16))
    for p in range(k // 512):
        a[p, :8] = np.random.permutation(np.resize(levels, 8))
        for g in range(8):
            far = levels[np.abs(levels - a[p, g]) >= 10]
            a[p, g + 8] = far[np.random.randint(len(far))]
    return np.exp2(a.ravel()).repeat(32)


def f64(x):
    return np.asarray(x).astype(np.float64)


def striped(idx):
    return np.tile(np.asarray(idx).reshape(-1, 16).T, (8, 1)).astype(np.uint16)


def unstriped(offs):
    return offs[:16].T.reshape(-1).astype(np.int64)


E2M1 = np.array([0.0, 0.5, 1.0, 1.5, 2.0, 3.0, 4.0, 6.0, -0.0, -0.5, -1.0, -1.5, -2.0, -3.0, -4.0, -6.0])


def pack_weight(w, fmt):
    k, n = w.shape
    w = f64(np.asarray(w, np.float32).astype(ml_dtypes.bfloat16)).reshape(k // 32, 32, n)
    amax = np.abs(w).max(1)
    if fmt == "e4m3":
        byte = np.frexp(amax)[1] - 1 + 127 - 7
    else:
        mant, ex = np.frexp(amax / 6.0)
        byte = np.where(mant > 0.5, ex, ex - 1) + 127
    byte = np.clip(np.where(amax > 0, byte, 1), 1, 254)
    scaled = (w * np.exp2(127.0 - byte)[:, None, :]).reshape(k, n).astype(np.float32)
    by_word = np.ascontiguousarray(scaled.reshape(k // 512, 128, 4, n).transpose(0, 1, 3, 2))
    if fmt == "e4m3":
        words = by_word.astype(ml_dtypes.float8_e4m3fn).view(np.uint8)
    else:
        c = by_word.astype(ml_dtypes.float4_e2m1fn).view(np.uint8) & 0xF
        words = (c[..., 0::2] | (c[..., 1::2] << 4)).reshape(k // 512, 128, 2 * n)
    return np.ascontiguousarray(words), np.ascontiguousarray(byte.astype(np.uint8).reshape(k // 512, 16, n))


def unpack_weight(words, scales, fmt):
    g, _, n = scales.shape
    words = np.ascontiguousarray(words).reshape(g, 128, n, -1)
    if fmt == "e4m3":
        vals = words.view(ml_dtypes.float8_e4m3fn).astype(np.float64)
    else:
        nib = np.empty((g, 128, n, 4), np.uint8)
        nib[..., 0::2] = words & 0xF
        nib[..., 1::2] = words >> 4
        vals = E2M1[nib]
    vals = vals * np.repeat(np.exp2(scales.astype(np.float64) - 127.0), 8, axis=1)[..., None]
    return vals.transpose(0, 1, 3, 2).reshape(g * 512, n)


D, T, I, J, E = 512, 2048, 512, 512, 512


def setup_inputs():
    n = np.random.standard_normal
    idx = np.random.permutation(T)[:I]
    idx2 = np.random.permutation(T)[:J]
    fd = mx_kscale(D)
    fj = mx_kscale(J)
    tj = np.ones(T)
    tj[idx2] = fj
    qpoolp = pack_weight(n((D, T)) * 0.5 / np.sqrt(D) * fd[:, None], "e4m3")
    keysp = pack_weight(n((D, T)) / fd[:, None], "e4m3")
    return {
        "qpool_words": qpoolp[0],
        "qpool_scales": qpoolp[1],
        "keys_words": keysp[0],
        "keys_scales": keysp[1],
        "vals": (n((E, T)) / tj).astype(np.float32),
        "mask": (0.5 * n((I, J))).astype(np.float32),
        "size": (np.random.uniform(0.5, 2.0, (1, J)) * fj).astype(np.float32),
        "offs": striped(idx),
        "offs2": striped(idx2),
    }


def reference(qpool_words, qpool_scales, keys_words, keys_scales, vals, mask, size, offs, offs2):
    idx = unstriped(offs)
    idx2 = unstriped(offs2)
    qpoolu = unpack_weight(qpool_words, qpool_scales, "e4m3")
    keysu = unpack_weight(keys_words, keys_scales, "e4m3")
    qpoolidxg = qpoolu[:, idx]
    keysidx2g = keysu[:, idx2]
    a = qpoolidxg.T @ keysidx2g
    s = a + f64(mask)
    p = np.exp(s - np.max(s, axis=1, keepdims=True))
    w = p * f64(size) / np.sum(p, axis=1, keepdims=True)
    wt = w.T
    vt = f64(vals)[:, idx2].T
    vtq = mxq(vt, 0, "e4m3")
    wtq = mxq(wt, 0, "e4m3")
    o = vtq.T @ wtq
    y = np.zeros((E, T))
    y[:, idx] = o
    return y

@@ -1,0 +1,206 @@
+from contextlib import ExitStack
+
+import concourse.mybir as mybir
+from concourse.masks import make_identity
+
+D, T, I, J, E = 512, 2048, 512, 512, 512
+FLOPS = 2 * D * I * J + 2 * J * E * I
+
+F32 = mybir.dt.float32
+BF16 = mybir.dt.bfloat16
+I32 = mybir.dt.int32
+U32 = mybir.dt.uint32
+U16 = mybir.dt.uint16
+U8 = mybir.dt.uint8
+FP8X4 = mybir.dt.float8_e4m3fn_x4
+ALU = mybir.AluOpType
+ACT = mybir.ActivationFunctionType
+
+P = 128
+TILES = 4
+CAST = 512
+HALF = 256
+
+
+def tile_attend_pickboth_kernel(tc, qpool_words, qpool_scales, keys_words, keys_scales, vals, mask, size, offs, offs2, out):
+    nc = tc.nc
+    with ExitStack() as ctx:
+        keep = ctx.enter_context(tc.tile_pool(name="keep", bufs=1))
+        psum = ctx.enter_context(tc.psum_pool(name="psum", bufs=1))
+
+        def load_words(tile, words):
+            nc.sync.dma_start(tile[:], words[0].rearrange("p c r -> p (c r)").bitcast(I32))
+
+        def load_scales(tile, scales, quadrants):
+            rows = scales[0].bitcast(I32)
+            for q in quadrants:
+                nc.sync.dma_start(
+                    tile[32 * q : 32 * q + 32, :].bitcast(I32),
+                    rows[4 * q : 4 * q + 4, :].unsqueeze(0).to_broadcast([8, 4, T // 4]),
+                )
+
+        q_list = keep.tile([P, I // 16], U16, name="q_list")
+        k_list = keep.tile([P, J // 16], U16, name="k_list")
+        k_word_pool = keep.tile([P, T], I32, name="k_word_pool")
+        q_word_pool = keep.tile([P, T], I32, name="q_word_pool", tag="q_word_pool")
+        k_byte_pool = keep.tile([P, T], U8, name="k_byte_pool")
+        q_byte_pool = keep.tile([P, T], U8, name="q_byte_pool")
+        size_cols = keep.tile([P, 4], F32, name="size_cols")
+        mask_rows = [keep.tile([P, J], F32, name="mask_rows%d" % i, tag="mask_rows%d" % i) for i in range(TILES)]
+        val_pool = [keep.tile([P, T], F32, name="val_pool%d" % r, tag="val_pool%d" % r, align_bytes=64) for r in range(TILES)]
+
+        nc.sync.dma_start(k_list[:], offs2)
+        load_scales(k_byte_pool, keys_scales, range(4))
+        load_words(k_word_pool, keys_words)
+        nc.sync.dma_start(q_list[:], offs)
+        nc.sync.dma_start(size_cols[:], size[0].rearrange("(n m) -> n m", m=4))
+        load_scales(q_byte_pool, qpool_scales, range(4))
+        load_words(q_word_pool, qpool_words)
+        for i in (0, 1):
+            nc.sync.dma_start(mask_rows[i][:], mask[P * i : P * (i + 1), :])
+        for r in (0, 1, 2):
+            nc.sync.dma_start(val_pool[r][:], vals[P * r : P * (r + 1), :])
+        for i in (2, 3):
+            nc.sync.dma_start(mask_rows[i][:], mask[P * i : P * (i + 1), :])
+        nc.sync.dma_start(val_pool[3][:], vals[P * 3 : P * 4, :])
+
+        windows = [keep.tile([P, T], F32, name="window0")]
+        nc.vector.memset(windows[0][:].bitcast(I32), 0)
+        ident = keep.tile([P, P], F32, name="ident")
+        make_identity(nc, ident[:])
+
+        size_all = psum.tile([P, 4, P], F32, name="size_all", tag="bank7")
+        for m in range(4):
+            nc.tensor.transpose(size_all[:, m, :], size_cols[:, m : m + 1].to_broadcast([P, P]), ident[:])
+
+        k_words = keep.tile([P, J], U32, name="k_words", align_bytes=64)
+        k_bytes = keep.tile([P, J], U8, name="k_bytes", align_bytes=64)
+        q_words = keep.tile([P, I], U32, name="q_words", align_bytes=64)
+        q_bytes = keep.tile([P, I], U8, name="q_bytes", align_bytes=64)
+        nc.vector.tensor_copy(k_bytes[:], k_byte_pool[:].indirect(k_list[:]))
+        nc.vector.tensor_copy(k_words[:], k_word_pool[:].bitcast(U32).indirect(k_list[:]))
+        nc.vector.tensor_copy(q_bytes[:], q_byte_pool[:].indirect(q_list[:]))
+        scores = []
+        for half in range(2):
+            nc.vector.tensor_copy(
+                q_words[:, 256 * half : 256 * (half + 1)],
+                q_word_pool[:].bitcast(U32).indirect(q_list[:, 16 * half : 16 * (half + 1)]),
+            )
+            for i in (2 * half, 2 * half + 1):
+                bank = psum.tile([P, J], F32, name="score%d" % i, tag="bank%d" % i)
+                cols = slice(P * i, P * (i + 1))
+                nc.tensor.matmul_mx(
+                    out=bank[:],
+                    lhsT=q_words[:, cols].bitcast(FP8X4),
+                    lhsT_scale=q_bytes[:, cols],
+                    rhs=k_words[:].bitcast(FP8X4),
+                    rhs_scale=k_bytes[:],
+                    start=True,
+                    stop=True,
+                )
+                scores.append(bank)
+        windows.append(keep.tile([P, T], F32, name="window1", tag="q_word_pool"))
+        nc.gpsimd.memset(windows[1][:], 0.0)
+
+        def turn_pairs(rows, grouped_words, bank):
+            words = rows[:].bitcast(F32)
+            turned = psum.tile([P, 2, P], F32, name="turned", tag="bank%d" % bank)
+            for u in range(2):
+                nc.tensor.transpose(turned[:, u, :], words[:, u : 2 * P : 2], ident[:])
+            nc.scalar.copy(grouped_words.rearrange("p (c u) -> p c u", u=2), turned[:].rearrange("p u c -> p c u"))
+
+        def round_values(r):
+            rounded = keep.tile([P, T], BF16, name="rounded%d" % r)
+            for c in range(0, T, CAST):
+                nc.scalar.activation(rounded[:, c : c + CAST], val_pool[r][:, c : c + CAST], ACT.Copy)
+            return rounded
+
+        def gather_on_scalar(r, rounded, tag):
+            picked = keep.tile([P, J], BF16, name="picked%d" % r, tag=tag, align_bytes=64)
+            nc.scalar.activation(picked[:], rounded[:].indirect(k_list[:]), ACT.Copy)
+            return picked
+
+        def gather_on_vector(r, tag):
+            picked = keep.tile([P, J], BF16, name="picked%d" % r, tag=tag, align_bytes=64)
+            nc.vector.tensor_copy(picked[:], val_pool[r][:].indirect(k_list[:]))
+            return picked
+
+        def quantize_values(r, picked, bank, tag):
+            grouped = keep.tile([P, 4 * P], BF16, name="v_grouped%d" % r, align_bytes=64)
+            turn_pairs(picked, grouped[:].bitcast(F32), bank)
+            codes = keep.tile([P, P], U32, name="v_codes%d" % r, tag=tag, align_bytes=64)
+            scales = keep.tile([P, P], U8, name="v_scales%d" % r, align_bytes=64)
+            nc.vector.quantize_mx(out=codes[:].bitcast(FP8X4), scales=scales[:], in_=grouped[:])
+            return codes, scales
+
+        def scatter(r, operand, half, bank_number, tag):
+            codes, scales = operand
+            cols = slice(HALF * half, HALF * (half + 1))
+            bank = psum.tile([P, HALF], F32, name="product%d" % r, tag="bank%d" % bank_number)
+            nc.tensor.matmul_mx(
+                out=bank[:],
+                lhsT=codes[:].bitcast(FP8X4),
+                lhsT_scale=scales[:],
+                rhs=w_codes[:, cols].bitcast(FP8X4),
+                rhs_scale=w_scales[:, cols],
+                start=True,
+                stop=True,
+            )
+            result = keep.tile([P, HALF], F32, name=tag + "_result", tag=tag, align_bytes=64)
+            nc.scalar.copy(result[:], bank[:])
+            nc.vector.tensor_copy(windows[r][:].indirect(q_list[:, 16 * half : 16 * (half + 1)]), result[:])
+            if half == 1:
+                nc.sync.dma_start(out[P * r : P * (r + 1), :], windows[r][:])
+
+        w_codes = keep.tile([P, I], U32, name="w_codes", align_bytes=64)
+        w_scales = keep.tile([P, I], U8, name="w_scales", align_bytes=64)
+
+        def weights(i, w_grouped):
+            s = keep.tile([P, J], F32, name="s%d" % i)
+            neg_max = keep.tile([P, 1], F32, name="neg_max%d" % i)
+            p = keep.tile([P, J], F32, name="p%d" % i, tag="p%d" % i, align_bytes=64)
+            total = keep.tile([P, 1], F32, name="total%d" % i, tag="total%d" % i, align_bytes=64)
+            inverse = keep.tile([P, 1], F32, name="inverse%d" % i)
+            w = keep.tile([P, J], BF16, name="w%d" % i, tag="w%d" % i, align_bytes=64)
+            nc.vector.tensor_tensor(s[:], scores[i][:], mask_rows[i][:], ALU.add)
+            nc.vector.tensor_reduce(neg_max[:], s[:], mybir.AxisListType.X, ALU.max, negate=True)
+            nc.scalar.activation(p[:], s[:], ACT.Exp, bias=neg_max[:], accum_out=total[:])
+            nc.vector.reciprocal(inverse[:], total[:])
+            nc.vector.scalar_tensor_tensor(
+                w[:].rearrange("p (n m) -> p n m", m=4),
+                p[:].rearrange("p (n m) -> p n m", m=4),
+                inverse[:],
+                size_all[:].rearrange("p m n -> p n m"),
+                ALU.mult,
+                ALU.mult,
+            )
+            turn_pairs(w, w_grouped[:].bitcast(F32)[:, 2 * P * (i % 2) : 2 * P * (i % 2 + 1)], 4 + i % 3)
+
+        def quantize_weights(half, w_grouped):
+            cols = slice(2 * P * half, 2 * P * (half + 1))
+            nc.vector.quantize_mx(out=w_codes[:, cols].bitcast(FP8X4), scales=w_scales[:, cols], in_=w_grouped[:])
+
+        w_first = keep.tile([P, 2 * I], BF16, name="w_first", align_bytes=64)
+        w_second = keep.tile([P, 2 * I], BF16, name="w_second", tag="w_second", align_bytes=64)
+        for i in (0, 1):
+            weights(i, w_first)
+            windows.append(keep.tile([P, T], F32, name="window%d" % (2 + i), tag="mask_rows%d" % i))
+            nc.gpsimd.memset(windows[2 + i][:], 0.0)
+        v0 = quantize_values(0, gather_on_vector(0, "picked0"), 0, "v_codes0")
+        quantize_weights(0, w_first)
+        picked1 = gather_on_scalar(1, round_values(1), "picked1")
+        picked2 = gather_on_vector(2, "picked2")
+        weights(2, w_second)
+        weights(3, w_second)
+        v2 = quantize_values(2, picked2, 2, "v_codes2")
+        v1 = quantize_values(1, picked1, 3, "v_codes1")
+        scatter(0, v0, 0, 1, "total3")
+        quantize_weights(1, w_second)
+        scatter(2, v2, 0, 0, "w3")
+        scatter(1, v1, 0, 6, "w_second")
+        scatter(0, v0, 1, 1, "result0")
+        v3 = quantize_values(3, gather_on_scalar(3, round_values(3), "picked3"), 5, "v_codes3")
+        scatter(1, v1, 1, 2, "picked3")
+        scatter(2, v2, 1, 5, "result2")
+        scatter(3, v3, 0, 3, "result3")
+        scatter(3, v3, 1, 0, "result4")

@@ -47,7 +47,8 @@ def tile_attend_pickboth_kernel(tc, qpool_words, qpool_scales, keys_words, keys_
         q_byte_pool = keep.tile([P, T], U8, name="q_byte_pool")
         size_cols = keep.tile([P, 4], F32, name="size_cols")
         mask_rows = [keep.tile([P, J], F32, name="mask_rows%d" % i, tag="mask_rows%d" % i) for i in range(TILES)]
-        val_pool = [keep.tile([P, T], F32, name="val_pool%d" % r, tag="val_pool%d" % r, align_bytes=64) for r in range(TILES)]
+        val_pool = [keep.tile([P, T], F32, name="val_pool%d" % r, tag="val_pool%d" % r, align_bytes=64) for r in range(TILES - 1)]
+        last_pool = [keep.tile([P, T // 2], F32, name="last_pool%d" % h, tag="last_pool%d" % h, align_bytes=64) for h in range(2)]
 
         nc.sync.dma_start(k_list[:], offs2)
         load_scales(k_byte_pool, keys_scales, range(4))
@@ -56,16 +57,19 @@ def tile_attend_pickboth_kernel(tc, qpool_words, qpool_scales, keys_words, keys_
         nc.sync.dma_start(size_cols[:], size[0].rearrange("(n m) -> n m", m=4))
         load_scales(q_byte_pool, qpool_scales, range(4))
         load_words(q_word_pool, qpool_words)
-        for i in (0, 1):
-            nc.sync.dma_start(mask_rows[i][:], mask[P * i : P * (i + 1), :])
-        for r in (0, 1, 2):
-            nc.sync.dma_start(val_pool[r][:], vals[P * r : P * (r + 1), :])
-        for i in (2, 3):
-            nc.sync.dma_start(mask_rows[i][:], mask[P * i : P * (i + 1), :])
-        nc.sync.dma_start(val_pool[3][:], vals[P * 3 : P * 4, :])
+        nc.sync.dma_start(mask_rows[0][:], mask[P * 0 : P * 1, :])
+        nc.sync.dma_start(mask_rows[1][:], mask[P * 1 : P * 2, :])
+        nc.sync.dma_start(val_pool[0][:], vals[P * 0 : P * 1, :])
+        nc.sync.dma_start(mask_rows[2][:], mask[P * 2 : P * 3, :])
+        nc.sync.dma_start(mask_rows[3][:], mask[P * 3 : P * 4, :])
+        nc.sync.dma_start(val_pool[1][:], vals[P * 1 : P * 2, :])
+        nc.sync.dma_start(val_pool[2][:], vals[P * 2 : P * 3, :])
+        for h in range(2):
+            nc.sync.dma_start(last_pool[h][:], vals[P * 3 : P * 4, T // 2 * h : T // 2 * (h + 1)])
 
-        windows = [keep.tile([P, T], F32, name="window0")]
-        nc.vector.memset(windows[0][:].bitcast(I32), 0)
+        windows = [keep.tile([P, T], F32, name="window%d" % b) for b in range(3)]
+        for window in windows:
+            nc.vector.memset(window[:].bitcast(I32), 0)
         ident = keep.tile([P, P], F32, name="ident")
         make_identity(nc, ident[:])
 
@@ -99,8 +103,6 @@ def tile_attend_pickboth_kernel(tc, qpool_words, qpool_scales, keys_words, keys_
                     stop=True,
                 )
                 scores.append(bank)
-        windows.append(keep.tile([P, T], F32, name="window1", tag="q_word_pool"))
-        nc.gpsimd.memset(windows[1][:], 0.0)
 
         def turn_pairs(rows, grouped_words, bank):
             words = rows[:].bitcast(F32)
@@ -109,10 +111,11 @@ def tile_attend_pickboth_kernel(tc, qpool_words, qpool_scales, keys_words, keys_
                 nc.tensor.transpose(turned[:, u, :], words[:, u : 2 * P : 2], ident[:])
             nc.scalar.copy(grouped_words.rearrange("p (c u) -> p c u", u=2), turned[:].rearrange("p u c -> p c u"))
 
-        def round_values(r):
+        def round_values(r, parts):
             rounded = keep.tile([P, T], BF16, name="rounded%d" % r)
+            width = T // len(parts)
             for c in range(0, T, CAST):
-                nc.scalar.activation(rounded[:, c : c + CAST], val_pool[r][:, c : c + CAST], ACT.Copy)
+                nc.scalar.activation(rounded[:, c : c + CAST], parts[c // width][:, c % width : c % width + CAST], ACT.Copy)
             return rounded
 
         def gather_on_scalar(r, rounded, tag):
@@ -125,43 +128,44 @@ def tile_attend_pickboth_kernel(tc, qpool_words, qpool_scales, keys_words, keys_
             nc.vector.tensor_copy(picked[:], val_pool[r][:].indirect(k_list[:]))
             return picked
 
-        def quantize_values(r, picked, bank, tag):
-            grouped = keep.tile([P, 4 * P], BF16, name="v_grouped%d" % r, align_bytes=64)
+        def quantize_values(r, picked, bank, grouped_tag, tag):
+            grouped = keep.tile([P, 4 * P], BF16, name="v_grouped%d" % r, tag=grouped_tag, align_bytes=64)
             turn_pairs(picked, grouped[:].bitcast(F32), bank)
             codes = keep.tile([P, P], U32, name="v_codes%d" % r, tag=tag, align_bytes=64)
             scales = keep.tile([P, P], U8, name="v_scales%d" % r, align_bytes=64)
             nc.vector.quantize_mx(out=codes[:].bitcast(FP8X4), scales=scales[:], in_=grouped[:])
             return codes, scales
 
-        def scatter(r, operand, half, bank_number, tag):
+        def scatter(r, operand, halves, bank_number, tag, window):
             codes, scales = operand
-            cols = slice(HALF * half, HALF * (half + 1))
-            bank = psum.tile([P, HALF], F32, name="product%d" % r, tag="bank%d" % bank_number)
-            nc.tensor.matmul_mx(
-                out=bank[:],
-                lhsT=codes[:].bitcast(FP8X4),
-                lhsT_scale=scales[:],
-                rhs=w_codes[:, cols].bitcast(FP8X4),
-                rhs_scale=w_scales[:, cols],
-                start=True,
-                stop=True,
-            )
-            result = keep.tile([P, HALF], F32, name=tag + "_result", tag=tag, align_bytes=64)
+            count = HALF * len(halves)
+            bank = psum.tile([P, count], F32, name="product%d" % r, tag="bank%d" % bank_number)
+            for n, half in enumerate(halves):
+                nc.tensor.matmul_mx(
+                    out=bank[:, HALF * n : HALF * (n + 1)],
+                    lhsT=codes[:].bitcast(FP8X4),
+                    lhsT_scale=scales[:],
+                    rhs=w_codes[half][:].bitcast(FP8X4),
+                    rhs_scale=w_scales[half][:],
+                    start=True,
+                    stop=True,
+                )
+            result = keep.tile([P, count], F32, name=tag + "_result", tag=tag, align_bytes=64)
             nc.scalar.copy(result[:], bank[:])
-            nc.vector.tensor_copy(windows[r][:].indirect(q_list[:, 16 * half : 16 * (half + 1)]), result[:])
-            if half == 1:
-                nc.sync.dma_start(out[P * r : P * (r + 1), :], windows[r][:])
+            nc.vector.tensor_copy(window[:].indirect(q_list[:, 16 * halves[0] : 16 * (halves[-1] + 1)]), result[:])
+            if halves[-1] == 1:
+                nc.sync.dma_start(out[P * r : P * (r + 1), :], window[:])
 
-        w_codes = keep.tile([P, I], U32, name="w_codes", align_bytes=64)
-        w_scales = keep.tile([P, I], U8, name="w_scales", align_bytes=64)
+        w_codes = {}
+        w_scales = {}
 
-        def weights(i, w_grouped):
-            s = keep.tile([P, J], F32, name="s%d" % i)
+        def weights(i, w_grouped, tag):
+            s = keep.tile([P, J], F32, name="s%d" % i, tag="s%d" % i, align_bytes=64)
             neg_max = keep.tile([P, 1], F32, name="neg_max%d" % i)
             p = keep.tile([P, J], F32, name="p%d" % i, tag="p%d" % i, align_bytes=64)
             total = keep.tile([P, 1], F32, name="total%d" % i, tag="total%d" % i, align_bytes=64)
             inverse = keep.tile([P, 1], F32, name="inverse%d" % i)
-            w = keep.tile([P, J], BF16, name="w%d" % i, tag="w%d" % i, align_bytes=64)
+            w = keep.tile([P, J], BF16, name="w%d" % i, tag=tag, align_bytes=64)
             nc.vector.tensor_tensor(s[:], scores[i][:], mask_rows[i][:], ALU.add)
             nc.vector.tensor_reduce(neg_max[:], s[:], mybir.AxisListType.X, ALU.max, negate=True)
             nc.scalar.activation(p[:], s[:], ACT.Exp, bias=neg_max[:], accum_out=total[:])
@@ -176,31 +180,29 @@ def tile_attend_pickboth_kernel(tc, qpool_words, qpool_scales, keys_words, keys_
             )
             turn_pairs(w, w_grouped[:].bitcast(F32)[:, 2 * P * (i % 2) : 2 * P * (i % 2 + 1)], 4 + i % 3)
 
-        def quantize_weights(half, w_grouped):
-            cols = slice(2 * P * half, 2 * P * (half + 1))
-            nc.vector.quantize_mx(out=w_codes[:, cols].bitcast(FP8X4), scales=w_scales[:, cols], in_=w_grouped[:])
+        def quantize_weights(half, w_grouped, tag):
+            w_codes[half] = keep.tile([P, HALF], U32, name="w_codes%d" % half, tag=tag, align_bytes=64)
+            w_scales[half] = keep.tile([P, HALF], U8, name="w_scales%d" % half, align_bytes=64)
+            nc.vector.quantize_mx(out=w_codes[half][:].bitcast(FP8X4), scales=w_scales[half][:], in_=w_grouped[:])
 
         w_first = keep.tile([P, 2 * I], BF16, name="w_first", align_bytes=64)
         w_second = keep.tile([P, 2 * I], BF16, name="w_second", tag="w_second", align_bytes=64)
-        for i in (0, 1):
-            weights(i, w_first)
-            windows.append(keep.tile([P, T], F32, name="window%d" % (2 + i), tag="mask_rows%d" % i))
-            nc.gpsimd.memset(windows[2 + i][:], 0.0)
-        v0 = quantize_values(0, gather_on_vector(0, "picked0"), 0, "v_codes0")
-        quantize_weights(0, w_first)
-        picked1 = gather_on_scalar(1, round_values(1), "picked1")
+        weights(0, w_first, "w0")
+        weights(1, w_first, "w1")
+        picked1 = gather_on_vector(1, "picked1")
+        weights(2, w_second, "val_pool1")
+        quantize_weights(0, w_first, "w_codes0")
+        weights(3, w_second, "w3")
+        v0 = quantize_values(0, gather_on_scalar(0, round_values(0, [val_pool[0]]), "picked0"), 0, "g0", "v_codes0")
+        v1 = quantize_values(1, picked1, 1, "g1", "p3")
         picked2 = gather_on_vector(2, "picked2")
-        weights(2, w_second)
-        weights(3, w_second)
-        v2 = quantize_values(2, picked2, 2, "v_codes2")
-        v1 = quantize_values(1, picked1, 3, "v_codes1")
-        scatter(0, v0, 0, 1, "total3")
-        quantize_weights(1, w_second)
-        scatter(2, v2, 0, 0, "w3")
-        scatter(1, v1, 0, 6, "w_second")
-        scatter(0, v0, 1, 1, "result0")
-        v3 = quantize_values(3, gather_on_scalar(3, round_values(3), "picked3"), 5, "v_codes3")
-        scatter(1, v1, 1, 2, "picked3")
-        scatter(2, v2, 1, 5, "result2")
-        scatter(3, v3, 0, 3, "result3")
-        scatter(3, v3, 1, 0, "result4")
+        scatter(0, v0, [0], 0, "result1", windows[0])
+        quantize_weights(1, w_second, "val_pool2")
+        scatter(1, v1, [0], 5, "result0", windows[1])
+        rounded3 = round_values(3, last_pool)
+        v2 = quantize_values(2, picked2, 2, "last_pool0", "v_codes2")
+        scatter(0, v0, [1], 1, "last_pool1", windows[0])
+        scatter(1, v1, [1], 1, "result3", windows[1])
+        v3 = quantize_values(3, gather_on_scalar(3, rounded3, "picked3"), 3, "g3", "v_codes3")
+        scatter(2, v2, [0, 1], 2, "picked3", windows[2])
+        scatter(3, v3, [0, 1], 5, "result6", windows[0])

@@ -31,13 +31,11 @@ def tile_attend_pickboth_kernel(tc, qpool_words, qpool_scales, keys_words, keys_
         def load_words(tile, words):
             nc.sync.dma_start(tile[:], words[0].rearrange("p c r -> p (c r)").bitcast(I32))
 
-        def load_scales(tile, scales, quadrants):
+        def load_scales(tile, scales, first):
+            nc.vector.memset(tile[:].bitcast(I32), 0)
             rows = scales[0].bitcast(I32)
-            for q in quadrants:
-                nc.sync.dma_start(
-                    tile[32 * q : 32 * q + 32, :].bitcast(I32),
-                    rows[4 * q : 4 * q + 4, :].unsqueeze(0).to_broadcast([8, 4, T // 4]),
-                )
+            for q in range(4):
+                nc.sync.dma_start(tile[32 * q + first : 32 * q + first + 4, :].bitcast(I32), rows[4 * q : 4 * q + 4, :])
 
         q_list = keep.tile([P, I // 16], U16, name="q_list")
         k_list = keep.tile([P, J // 16], U16, name="k_list")
@@ -51,12 +49,12 @@ def tile_attend_pickboth_kernel(tc, qpool_words, qpool_scales, keys_words, keys_
         last_pool = [keep.tile([P, T // 2], F32, name="last_pool%d" % h, tag="last_pool%d" % h, align_bytes=64) for h in range(2)]
 
         nc.sync.dma_start(k_list[:], offs2)
-        load_scales(k_byte_pool, keys_scales, range(4))
-        load_words(k_word_pool, keys_words)
         nc.sync.dma_start(q_list[:], offs)
         nc.sync.dma_start(size_cols[:], size[0].rearrange("(n m) -> n m", m=4))
-        load_scales(q_byte_pool, qpool_scales, range(4))
+        load_words(k_word_pool, keys_words)
+        load_scales(k_byte_pool, keys_scales, 0)
         load_words(q_word_pool, qpool_words)
+        load_scales(q_byte_pool, qpool_scales, 4)
         nc.sync.dma_start(mask_rows[0][:], mask[P * 0 : P * 1, :])
         nc.sync.dma_start(mask_rows[1][:], mask[P * 1 : P * 2, :])
         nc.sync.dma_start(val_pool[0][:], vals[P * 0 : P * 1, :])
@@ -81,14 +79,17 @@ def tile_attend_pickboth_kernel(tc, qpool_words, qpool_scales, keys_words, keys_
         k_bytes = keep.tile([P, J], U8, name="k_bytes", align_bytes=64)
         q_words = keep.tile([P, I], U32, name="q_words", align_bytes=64)
         q_bytes = keep.tile([P, I], U8, name="q_bytes", align_bytes=64)
-        nc.vector.tensor_copy(k_bytes[:], k_byte_pool[:].indirect(k_list[:]))
         nc.vector.tensor_copy(k_words[:], k_word_pool[:].bitcast(U32).indirect(k_list[:]))
-        nc.vector.tensor_copy(q_bytes[:], q_byte_pool[:].indirect(q_list[:]))
+        nc.vector.tensor_copy(k_bytes[:], k_byte_pool[:].indirect(k_list[:]))
         scores = []
         for half in range(2):
             nc.vector.tensor_copy(
                 q_words[:, 256 * half : 256 * (half + 1)],
                 q_word_pool[:].bitcast(U32).indirect(q_list[:, 16 * half : 16 * (half + 1)]),
+            )
+            nc.vector.tensor_copy(
+                q_bytes[:, 256 * half : 256 * (half + 1)],
+                q_byte_pool[:].indirect(q_list[:, 16 * half : 16 * (half + 1)]),
             )
             for i in (2 * half, 2 * half + 1):
                 bank = psum.tile([P, J], F32, name="score%d" % i, tag="bank%d" % i)
@@ -96,7 +97,7 @@ def tile_attend_pickboth_kernel(tc, qpool_words, qpool_scales, keys_words, keys_
                 nc.tensor.matmul_mx(
                     out=bank[:],
                     lhsT=q_words[:, cols].bitcast(FP8X4),
-                    lhsT_scale=q_bytes[:, cols],
+                    lhsT_scale=q_bytes[4:P, cols],
                     rhs=k_words[:].bitcast(FP8X4),
                     rhs_scale=k_bytes[:],
                     start=True,

@@ -42,22 +42,24 @@ def tile_attend_pickboth_kernel(tc, qpool_words, qpool_scales, keys_words, keys_
         k_word_pool = keep.tile([P, T], I32, name="k_word_pool")
         q_word_pool = keep.tile([P, T], I32, name="q_word_pool", tag="q_word_pool")
         k_byte_pool = keep.tile([P, T], U8, name="k_byte_pool")
-        q_byte_pool = keep.tile([P, T], U8, name="q_byte_pool")
+        q_byte_pool = keep.tile([P, T], U8, name="q_byte_pool", tag="q_byte_pool", align_bytes=64)
         size_cols = keep.tile([P, 4], F32, name="size_cols")
         mask_rows = [keep.tile([P, J], F32, name="mask_rows%d" % i, tag="mask_rows%d" % i) for i in range(TILES)]
-        val_pool = [keep.tile([P, T], F32, name="val_pool%d" % r, tag="val_pool%d" % r, align_bytes=64) for r in range(TILES - 1)]
+        val_pool = {r: keep.tile([P, T], F32, name="val_pool%d" % r, tag="val_pool%d" % r, align_bytes=64) for r in (1, 2)}
+        first_pool = [keep.tile([P, T // 2], F32, name="first_pool%d" % h) for h in range(2)]
         last_pool = [keep.tile([P, T // 2], F32, name="last_pool%d" % h, tag="last_pool%d" % h, align_bytes=64) for h in range(2)]
 
         nc.sync.dma_start(k_list[:], offs2)
-        nc.sync.dma_start(q_list[:], offs)
-        nc.sync.dma_start(size_cols[:], size[0].rearrange("(n m) -> n m", m=4))
+        nc.scalar.dma_start(size_cols[:], size[0].rearrange("(n m) -> n m", m=4))
         load_words(k_word_pool, keys_words)
         load_scales(k_byte_pool, keys_scales, 0)
+        nc.sync.dma_start(q_list[:], offs)
         load_words(q_word_pool, qpool_words)
         load_scales(q_byte_pool, qpool_scales, 4)
+        nc.sync.dma_start(first_pool[0][:], vals[0:P, 0 : T // 2])
         nc.sync.dma_start(mask_rows[0][:], mask[P * 0 : P * 1, :])
         nc.sync.dma_start(mask_rows[1][:], mask[P * 1 : P * 2, :])
-        nc.sync.dma_start(val_pool[0][:], vals[P * 0 : P * 1, :])
+        nc.sync.dma_start(first_pool[1][:], vals[0:P, T // 2 : T])
         nc.sync.dma_start(mask_rows[2][:], mask[P * 2 : P * 3, :])
         nc.sync.dma_start(mask_rows[3][:], mask[P * 3 : P * 4, :])
         nc.sync.dma_start(val_pool[1][:], vals[P * 1 : P * 2, :])
@@ -74,36 +76,47 @@ def tile_attend_pickboth_kernel(tc, qpool_words, qpool_scales, keys_words, keys_
         size_all = psum.tile([P, 4, P], F32, name="size_all", tag="bank7")
         for m in range(4):
             nc.tensor.transpose(size_all[:, m, :], size_cols[:, m : m + 1].to_broadcast([P, P]), ident[:])
+        size_rows = keep.tile([P, J], F32, name="size_rows")
+        nc.scalar.copy(size_rows[:].rearrange("p (n m) -> p n m", m=4), size_all[:].rearrange("p m n -> p n m"))
 
         k_words = keep.tile([P, J], U32, name="k_words", align_bytes=64)
         k_bytes = keep.tile([P, J], U8, name="k_bytes", align_bytes=64)
-        q_words = keep.tile([P, I], U32, name="q_words", align_bytes=64)
         q_bytes = keep.tile([P, I], U8, name="q_bytes", align_bytes=64)
         nc.vector.tensor_copy(k_words[:], k_word_pool[:].bitcast(U32).indirect(k_list[:]))
         nc.vector.tensor_copy(k_bytes[:], k_byte_pool[:].indirect(k_list[:]))
         scores = []
-        for half in range(2):
+
+        def gather_query_words(half, tag):
+            words = keep.tile([P, HALF], U32, name="q_words%d" % half, tag=tag, align_bytes=64)
+            nc.vector.tensor_copy(words[:], q_word_pool[:].bitcast(U32).indirect(q_list[:, 16 * half : 16 * (half + 1)]))
+            return words
+
+        def gather_query_bytes(half):
             nc.vector.tensor_copy(
-                q_words[:, 256 * half : 256 * (half + 1)],
-                q_word_pool[:].bitcast(U32).indirect(q_list[:, 16 * half : 16 * (half + 1)]),
-            )
-            nc.vector.tensor_copy(
-                q_bytes[:, 256 * half : 256 * (half + 1)],
+                q_bytes[:, HALF * half : HALF * (half + 1)],
                 q_byte_pool[:].indirect(q_list[:, 16 * half : 16 * (half + 1)]),
             )
-            for i in (2 * half, 2 * half + 1):
+
+        def score(half, words):
+            for n in range(2):
+                i = 2 * half + n
                 bank = psum.tile([P, J], F32, name="score%d" % i, tag="bank%d" % i)
-                cols = slice(P * i, P * (i + 1))
                 nc.tensor.matmul_mx(
                     out=bank[:],
-                    lhsT=q_words[:, cols].bitcast(FP8X4),
-                    lhsT_scale=q_bytes[4:P, cols],
+                    lhsT=words[:, P * n : P * (n + 1)].bitcast(FP8X4),
+                    lhsT_scale=q_bytes[4:P, P * i : P * (i + 1)],
                     rhs=k_words[:].bitcast(FP8X4),
                     rhs_scale=k_bytes[:],
                     start=True,
                     stop=True,
                 )
                 scores.append(bank)
+
+        first_words = gather_query_words(0, "q_words0")
+        gather_query_bytes(0)
+        score(0, first_words)
+        gather_query_bytes(1)
+        score(1, gather_query_words(1, "q_byte_pool"))
 
         def turn_pairs(rows, grouped_words, bank):
             words = rows[:].bitcast(F32)
@@ -171,14 +184,7 @@ def tile_attend_pickboth_kernel(tc, qpool_words, qpool_scales, keys_words, keys_
             nc.vector.tensor_reduce(neg_max[:], s[:], mybir.AxisListType.X, ALU.max, negate=True)
             nc.scalar.activation(p[:], s[:], ACT.Exp, bias=neg_max[:], accum_out=total[:])
             nc.vector.reciprocal(inverse[:], total[:])
-            nc.vector.scalar_tensor_tensor(
-                w[:].rearrange("p (n m) -> p n m", m=4),
-                p[:].rearrange("p (n m) -> p n m", m=4),
-                inverse[:],
-                size_all[:].rearrange("p m n -> p n m"),
-                ALU.mult,
-                ALU.mult,
-            )
+            nc.vector.scalar_tensor_tensor(w[:], p[:], inverse[:], size_rows[:], ALU.mult, ALU.mult)
             turn_pairs(w, w_grouped[:].bitcast(F32)[:, 2 * P * (i % 2) : 2 * P * (i % 2 + 1)], 4 + i % 3)
 
         def quantize_weights(half, w_grouped, tag):
@@ -190,13 +196,13 @@ def tile_attend_pickboth_kernel(tc, qpool_words, qpool_scales, keys_words, keys_
         w_second = keep.tile([P, 2 * I], BF16, name="w_second", tag="w_second", align_bytes=64)
         weights(0, w_first, "w0")
         weights(1, w_first, "w1")
-        picked1 = gather_on_vector(1, "picked1")
+        picked1 = gather_on_vector(1, "p1")
         weights(2, w_second, "val_pool1")
         quantize_weights(0, w_first, "w_codes0")
         weights(3, w_second, "w3")
-        v0 = quantize_values(0, gather_on_scalar(0, round_values(0, [val_pool[0]]), "picked0"), 0, "g0", "v_codes0")
-        v1 = quantize_values(1, picked1, 1, "g1", "p3")
-        picked2 = gather_on_vector(2, "picked2")
+        v0 = quantize_values(0, gather_on_scalar(0, round_values(0, first_pool), "s1"), 0, "g0", "v_codes0")
+        v1 = quantize_values(1, picked1, 1, "g1", "v_codes1")
+        picked2 = gather_on_vector(2, "p3")
         scatter(0, v0, [0], 0, "result1", windows[0])
         quantize_weights(1, w_second, "val_pool2")
         scatter(1, v1, [0], 5, "result0", windows[1])

@@ -34,8 +34,8 @@ def tile_attend_pickboth_kernel(tc, qpool_words, qpool_scales, keys_words, keys_
         def load_scales(tile, scales, first):
             nc.vector.memset(tile[:].bitcast(I32), 0)
             rows = scales[0].bitcast(I32)
-            for q in range(4):
-                nc.sync.dma_start(tile[32 * q + first : 32 * q + first + 4, :].bitcast(I32), rows[4 * q : 4 * q + 4, :])
+            for m in range(4):
+                nc.sync.dma_start(tile[first + m : P : 32, :].bitcast(I32), rows[m:16:4, :])
 
         q_list = keep.tile([P, I // 16], U16, name="q_list")
         k_list = keep.tile([P, J // 16], U16, name="k_list")

@@ -20,6 +20,7 @@ P = 128
 TILES = 4
 CAST = 512
 HALF = 256
+ON_VECTOR = (1, 2)
 
 
 def tile_attend_pickboth_kernel(tc, qpool_words, qpool_scales, keys_words, keys_scales, vals, mask, size, offs, offs2, out):
@@ -28,50 +29,71 @@ def tile_attend_pickboth_kernel(tc, qpool_words, qpool_scales, keys_words, keys_
         keep = ctx.enter_context(tc.tile_pool(name="keep", bufs=1))
         psum = ctx.enter_context(tc.psum_pool(name="psum", bufs=1))
 
+        staged = ctx.enter_context(tc.tile_pool(name="staged", bufs=1))
+
+        def place(shape, dtype, name, where):
+            if isinstance(where, int):
+                return staged.tile(shape, dtype, name=name, offset=where, align_bytes=64)
+            return keep.tile(shape, dtype, name=name, tag=where, align_bytes=64)
+
         def load_words(tile, words):
             nc.sync.dma_start(tile[:], words[0].rearrange("p c r -> p (c r)").bitcast(I32))
 
-        def load_scales(tile, scales, first):
-            nc.vector.memset(tile[:].bitcast(I32), 0)
+        def load_scales(queue, tile, scales, first):
             rows = scales[0].bitcast(I32)
             for m in range(4):
-                nc.sync.dma_start(tile[first + m : P : 32, :].bitcast(I32), rows[m:16:4, :])
+                queue.dma_start(tile[first + m : P : 32, :].bitcast(I32), rows[m:16:4, :])
 
+        ROW = 4 * T
         q_list = keep.tile([P, I // 16], U16, name="q_list")
         k_list = keep.tile([P, J // 16], U16, name="k_list")
-        k_word_pool = keep.tile([P, T], I32, name="k_word_pool")
-        q_word_pool = keep.tile([P, T], I32, name="q_word_pool", tag="q_word_pool")
         k_byte_pool = keep.tile([P, T], U8, name="k_byte_pool")
         q_byte_pool = keep.tile([P, T], U8, name="q_byte_pool", tag="q_byte_pool", align_bytes=64)
         size_cols = keep.tile([P, 4], F32, name="size_cols")
-        mask_rows = [keep.tile([P, J], F32, name="mask_rows%d" % i, tag="mask_rows%d" % i) for i in range(TILES)]
-        val_pool = {r: keep.tile([P, T], F32, name="val_pool%d" % r, tag="val_pool%d" % r, align_bytes=64) for r in (1, 2)}
-        first_pool = [keep.tile([P, T // 2], F32, name="first_pool%d" % h) for h in range(2)]
-        last_pool = [keep.tile([P, T // 2], F32, name="last_pool%d" % h, tag="last_pool%d" % h, align_bytes=64) for h in range(2)]
+        k_word_pool = staged.tile([P, T], I32, name="k_word_pool", offset=0)
+        q_word_pool = staged.tile([P, T], I32, name="q_word_pool", offset=ROW)
+        mask_rows = [staged.tile([P, J], F32, name="mask_rows%d" % i, offset=2 * ROW + 4 * J * i) for i in range(TILES)]
+        val_pool = {r: staged.tile([P, T], F32, name="val_pool%d" % r, offset=(3 + r) * ROW) for r in ON_VECTOR}
+        parts = {
+            r: [staged.tile([P, T // 2], F32, name="val%d_%d" % (r, h), offset=(3 + r) * ROW + ROW // 2 * h) for h in range(2)]
+            for r in range(TILES)
+            if r not in ON_VECTOR
+        }
 
+        def load_part(r, h):
+            nc.sync.dma_start(parts[r][h][:], vals[P * r : P * (r + 1), T // 2 * h : T // 2 * (h + 1)])
+
+        def load_mask(i):
+            nc.sync.dma_start(mask_rows[i][:], mask[P * i : P * (i + 1), :])
+
+        def load_values(r):
+            nc.sync.dma_start(val_pool[r][:], vals[P * r : P * (r + 1), :])
+
+        nc.vector.memset(k_byte_pool[:].bitcast(I32), 0)
+        nc.vector.memset(q_byte_pool[:].bitcast(I32), 0)
         nc.sync.dma_start(k_list[:], offs2)
         nc.scalar.dma_start(size_cols[:], size[0].rearrange("(n m) -> n m", m=4))
         load_words(k_word_pool, keys_words)
-        load_scales(k_byte_pool, keys_scales, 0)
+        load_scales(nc.sync, k_byte_pool, keys_scales, 0)
         nc.sync.dma_start(q_list[:], offs)
         load_words(q_word_pool, qpool_words)
-        load_scales(q_byte_pool, qpool_scales, 4)
-        nc.sync.dma_start(first_pool[0][:], vals[0:P, 0 : T // 2])
-        nc.sync.dma_start(mask_rows[0][:], mask[P * 0 : P * 1, :])
-        nc.sync.dma_start(mask_rows[1][:], mask[P * 1 : P * 2, :])
-        nc.sync.dma_start(first_pool[1][:], vals[0:P, T // 2 : T])
-        nc.sync.dma_start(mask_rows[2][:], mask[P * 2 : P * 3, :])
-        nc.sync.dma_start(mask_rows[3][:], mask[P * 3 : P * 4, :])
-        nc.sync.dma_start(val_pool[1][:], vals[P * 1 : P * 2, :])
-        nc.sync.dma_start(val_pool[2][:], vals[P * 2 : P * 3, :])
-        for h in range(2):
-            nc.sync.dma_start(last_pool[h][:], vals[P * 3 : P * 4, T // 2 * h : T // 2 * (h + 1)])
+        load_scales(nc.sync, q_byte_pool, qpool_scales, 4)
+        load_part(0, 0)
+        load_mask(0)
+        load_mask(1)
+        load_part(0, 1)
+        load_mask(2)
+        load_mask(3)
+        load_values(1)
+        load_values(2)
+        load_part(3, 0)
+        load_part(3, 1)
 
         windows = [keep.tile([P, T], F32, name="window%d" % b) for b in range(3)]
-        for window in windows:
-            nc.vector.memset(window[:].bitcast(I32), 0)
         ident = keep.tile([P, P], F32, name="ident")
         make_identity(nc, ident[:])
+        for window in windows:
+            nc.vector.memset(window[:].bitcast(I32), 0)
 
         size_all = psum.tile([P, 4, P], F32, name="size_all", tag="bank7")
         for m in range(4):
@@ -133,30 +155,35 @@ def tile_attend_pickboth_kernel(tc, qpool_words, qpool_scales, keys_words, keys_
             return rounded
 
         def gather_on_scalar(r, rounded, tag):
-            picked = keep.tile([P, J], BF16, name="picked%d" % r, tag=tag, align_bytes=64)
+            picked = place([P, J], BF16, "picked%d" % r, tag)
             nc.scalar.activation(picked[:], rounded[:].indirect(k_list[:]), ACT.Copy)
             return picked
 
+        def gather_half_on_scalar(picked, rounded, half):
+            nc.scalar.activation(
+                picked[:, HALF * half : HALF * (half + 1)], rounded[:].indirect(k_list[:, 16 * half : 16 * (half + 1)]), ACT.Copy
+            )
+
         def gather_on_vector(r, tag):
-            picked = keep.tile([P, J], BF16, name="picked%d" % r, tag=tag, align_bytes=64)
+            picked = place([P, J], BF16, "picked%d" % r, tag)
             nc.vector.tensor_copy(picked[:], val_pool[r][:].indirect(k_list[:]))
             return picked
 
         def quantize_values(r, picked, bank, grouped_tag, tag):
-            grouped = keep.tile([P, 4 * P], BF16, name="v_grouped%d" % r, tag=grouped_tag, align_bytes=64)
+            grouped = place([P, 4 * P], BF16, "v_grouped%d" % r, grouped_tag)
             turn_pairs(picked, grouped[:].bitcast(F32), bank)
-            codes = keep.tile([P, P], U32, name="v_codes%d" % r, tag=tag, align_bytes=64)
+            codes = place([P, P], U32, "v_codes%d" % r, tag)
             scales = keep.tile([P, P], U8, name="v_scales%d" % r, align_bytes=64)
             nc.vector.quantize_mx(out=codes[:].bitcast(FP8X4), scales=scales[:], in_=grouped[:])
             return codes, scales
 
-        def scatter(r, operand, halves, bank_number, tag, window):
+        def scatter(r, operand, halves, banks, tag, window):
             codes, scales = operand
-            count = HALF * len(halves)
-            bank = psum.tile([P, count], F32, name="product%d" % r, tag="bank%d" % bank_number)
+            result = place([P, HALF * len(halves)], F32, "result%d_%d" % (r, halves[0]), tag)
             for n, half in enumerate(halves):
+                bank = psum.tile([P, HALF], F32, name="product%d_%d" % (r, half), tag="bank%d" % banks[n])
                 nc.tensor.matmul_mx(
-                    out=bank[:, HALF * n : HALF * (n + 1)],
+                    out=bank[:],
                     lhsT=codes[:].bitcast(FP8X4),
                     lhsT_scale=scales[:],
                     rhs=w_codes[half][:].bitcast(FP8X4),
@@ -164,8 +191,7 @@ def tile_attend_pickboth_kernel(tc, qpool_words, qpool_scales, keys_words, keys_
                     start=True,
                     stop=True,
                 )
-            result = keep.tile([P, count], F32, name=tag + "_result", tag=tag, align_bytes=64)
-            nc.scalar.copy(result[:], bank[:])
+                nc.scalar.copy(result[:, HALF * n : HALF * (n + 1)], bank[:])
             nc.vector.tensor_copy(window[:].indirect(q_list[:, 16 * halves[0] : 16 * (halves[-1] + 1)]), result[:])
             if halves[-1] == 1:
                 nc.sync.dma_start(out[P * r : P * (r + 1), :], window[:])
@@ -173,43 +199,69 @@ def tile_attend_pickboth_kernel(tc, qpool_words, qpool_scales, keys_words, keys_
         w_codes = {}
         w_scales = {}
 
-        def weights(i, w_grouped, tag):
-            s = keep.tile([P, J], F32, name="s%d" % i, tag="s%d" % i, align_bytes=64)
-            neg_max = keep.tile([P, 1], F32, name="neg_max%d" % i)
-            p = keep.tile([P, J], F32, name="p%d" % i, tag="p%d" % i, align_bytes=64)
-            total = keep.tile([P, 1], F32, name="total%d" % i, tag="total%d" % i, align_bytes=64)
-            inverse = keep.tile([P, 1], F32, name="inverse%d" % i)
-            w = keep.tile([P, J], BF16, name="w%d" % i, tag=tag, align_bytes=64)
-            nc.vector.tensor_tensor(s[:], scores[i][:], mask_rows[i][:], ALU.add)
-            nc.vector.tensor_reduce(neg_max[:], s[:], mybir.AxisListType.X, ALU.max, negate=True)
-            nc.scalar.activation(p[:], s[:], ACT.Exp, bias=neg_max[:], accum_out=total[:])
-            nc.vector.reciprocal(inverse[:], total[:])
-            nc.vector.scalar_tensor_tensor(w[:], p[:], inverse[:], size_rows[:], ALU.mult, ALU.mult)
+        s = {}
+        p = {}
+        neg_max = {}
+        total = {}
+        inverse = {}
+
+        def add_mask(i, tag):
+            s[i] = place([P, J], F32, "s%d" % i, tag)
+            nc.vector.tensor_tensor(s[i][:], scores[i][:], mask_rows[i][:], ALU.add)
+
+        def exponentiate(i, tag, p_tag):
+            neg_max[i] = place([P, 1], F32, "neg_max%d" % i, tag)
+            p[i] = place([P, J], F32, "p%d" % i, p_tag)
+            total[i] = keep.tile([P, 1], F32, name="total%d" % i, tag="total%d" % i, align_bytes=64)
+            nc.vector.tensor_reduce(neg_max[i][:], s[i][:], mybir.AxisListType.X, ALU.max, negate=True)
+            nc.scalar.activation(p[i][:], s[i][:], ACT.Exp, bias=neg_max[i][:], accum_out=total[i][:])
+
+        def invert(i, tag):
+            inverse[i] = place([P, 1], F32, "inverse%d" % i, tag)
+            nc.vector.reciprocal(inverse[i][:], total[i][:])
+
+        def weigh(i, w_grouped, tag):
+            w = place([P, J], BF16, "w%d" % i, tag)
+            nc.vector.scalar_tensor_tensor(w[:], p[i][:], inverse[i][:], size_rows[:], ALU.mult, ALU.mult)
             turn_pairs(w, w_grouped[:].bitcast(F32)[:, 2 * P * (i % 2) : 2 * P * (i % 2 + 1)], 4 + i % 3)
 
         def quantize_weights(half, w_grouped, tag):
-            w_codes[half] = keep.tile([P, HALF], U32, name="w_codes%d" % half, tag=tag, align_bytes=64)
+            w_codes[half] = place([P, HALF], U32, "w_codes%d" % half, tag)
             w_scales[half] = keep.tile([P, HALF], U8, name="w_scales%d" % half, align_bytes=64)
             nc.vector.quantize_mx(out=w_codes[half][:].bitcast(FP8X4), scales=w_scales[half][:], in_=w_grouped[:])
 
         w_first = keep.tile([P, 2 * I], BF16, name="w_first", align_bytes=64)
         w_second = keep.tile([P, 2 * I], BF16, name="w_second", tag="w_second", align_bytes=64)
-        weights(0, w_first, "w0")
-        weights(1, w_first, "w1")
-        picked1 = gather_on_vector(1, "p1")
-        weights(2, w_second, "val_pool1")
-        quantize_weights(0, w_first, "w_codes0")
-        weights(3, w_second, "w3")
-        v0 = quantize_values(0, gather_on_scalar(0, round_values(0, first_pool), "s1"), 0, "g0", "v_codes0")
+        last_window = staged.tile([P, T], F32, name="last_window", offset=ROW)
+        nc.gpsimd.memset(last_window[:].bitcast(I32), 0)
+        add_mask(0, "s0")
+        add_mask(1, "s1")
+        exponentiate(0, "m0", "p0")
+        exponentiate(1, "m1", "p1")
+        add_mask(2, "s2")
+        add_mask(3, "s3")
+        invert(0, "i0")
+        exponentiate(2, "m2", "p2")
+        weigh(0, w_first, "w0")
+        invert(1, "i1")
+        exponentiate(3, "m3", "p3")
+        weigh(1, w_first, "w1")
+        picked1 = gather_on_vector(1, "p0")
+        invert(2, "i2")
+        v0 = quantize_values(0, gather_on_scalar(0, round_values(0, parts[0]), "s1"), 0, "g0", "v_codes0")
+        weigh(2, w_second, 4 * ROW)
+        invert(3, 4 * ROW + 1024)
+        quantize_weights(0, w_first, 4 * ROW + 2048)
+        weigh(3, w_second, "w3")
         v1 = quantize_values(1, picked1, 1, "g1", "v_codes1")
-        picked2 = gather_on_vector(2, "p3")
-        scatter(0, v0, [0], 0, "result1", windows[0])
-        quantize_weights(1, w_second, "val_pool2")
-        scatter(1, v1, [0], 5, "result0", windows[1])
-        rounded3 = round_values(3, last_pool)
-        v2 = quantize_values(2, picked2, 2, "last_pool0", "v_codes2")
-        scatter(0, v0, [1], 1, "last_pool1", windows[0])
-        scatter(1, v1, [1], 1, "result3", windows[1])
+        picked2 = gather_on_vector(2, "p2")
+        scatter(0, v0, [0], [0], "w2x", windows[0])
+        quantize_weights(1, w_second, 5 * ROW)
+        scatter(1, v1, [0], [5], "result0", windows[1])
+        rounded3 = round_values(3, parts[3])
+        v2 = quantize_values(2, picked2, 2, 6 * ROW, "v_codes2")
+        scatter(0, v0, [1], [1], 6 * ROW + ROW // 2, windows[0])
+        scatter(1, v1, [1], [1], "result3", windows[1])
         v3 = quantize_values(3, gather_on_scalar(3, rounded3, "picked3"), 3, "g3", "v_codes3")
-        scatter(2, v2, [0, 1], 2, "picked3", windows[2])
-        scatter(3, v3, [0, 1], 5, "result6", windows[0])
+        scatter(2, v2, [0, 1], [2, 0], "picked3", windows[2])
+        scatter(3, v3, [0, 1], [5, 6], "result6", last_window)

@@ -17,10 +17,9 @@ ALU = mybir.AluOpType
 ACT = mybir.ActivationFunctionType
 
 P = 128
-TILES = 4
 CAST = 512
 HALF = 256
-ON_VECTOR = (1, 2)
+ROW = 4 * T
 
 
 def tile_attend_pickboth_kernel(tc, qpool_words, qpool_scales, keys_words, keys_scales, vals, mask, size, offs, offs2, out):
@@ -28,240 +27,227 @@ def tile_attend_pickboth_kernel(tc, qpool_words, qpool_scales, keys_words, keys_
     with ExitStack() as ctx:
         keep = ctx.enter_context(tc.tile_pool(name="keep", bufs=1))
         psum = ctx.enter_context(tc.psum_pool(name="psum", bufs=1))
-
         staged = ctx.enter_context(tc.tile_pool(name="staged", bufs=1))
 
-        def place(shape, dtype, name, where):
+        def place(shape, dtype, name, where=None):
             if isinstance(where, int):
                 return staged.tile(shape, dtype, name=name, offset=where, align_bytes=64)
-            return keep.tile(shape, dtype, name=name, tag=where, align_bytes=64)
+            return keep.tile(shape, dtype, name=name, tag=where or name, align_bytes=64)
+
+        def bank(shape, name, number):
+            return psum.tile(shape, F32, name=name, tag="bank%d" % number)
 
         def load_words(tile, words):
             nc.sync.dma_start(tile[:], words[0].rearrange("p c r -> p (c r)").bitcast(I32))
 
-        def load_scales(queue, tile, scales, first):
+        def load_scales(tile, scales, first):
             rows = scales[0].bitcast(I32)
             for m in range(4):
-                queue.dma_start(tile[first + m : P : 32, :].bitcast(I32), rows[m:16:4, :])
+                nc.sync.dma_start(tile[first + m : P : 32, :].bitcast(I32), rows[m:16:4, :])
 
-        ROW = 4 * T
         q_list = keep.tile([P, I // 16], U16, name="q_list")
         k_list = keep.tile([P, J // 16], U16, name="k_list")
-        k_byte_pool = keep.tile([P, T], U8, name="k_byte_pool")
-        q_byte_pool = keep.tile([P, T], U8, name="q_byte_pool", tag="q_byte_pool", align_bytes=64)
-        size_cols = keep.tile([P, 4], F32, name="size_cols")
-        k_word_pool = staged.tile([P, T], I32, name="k_word_pool", offset=0)
-        q_word_pool = staged.tile([P, T], I32, name="q_word_pool", offset=ROW)
-        mask_rows = [staged.tile([P, J], F32, name="mask_rows%d" % i, offset=2 * ROW + 4 * J * i) for i in range(TILES)]
-        val_pool = {r: staged.tile([P, T], F32, name="val_pool%d" % r, offset=(3 + r) * ROW) for r in ON_VECTOR}
-        parts = {
-            r: [staged.tile([P, T // 2], F32, name="val%d_%d" % (r, h), offset=(3 + r) * ROW + ROW // 2 * h) for h in range(2)]
-            for r in range(TILES)
-            if r not in ON_VECTOR
-        }
+        k_byte_pool = place([P, T], U8, "k_byte_pool")
+        q_byte_pool = place([P, T], U8, "q_byte_pool")
+        size_cols = place([P, 4], F32, "size_cols")
+        k_word_pool = place([P, T], I32, "k_word_pool", 0)
+        q_word_pool = place([P, T], I32, "q_word_pool", ROW)
+        mask_pair = place([P, 2, J], F32, "mask_pair")
+        mask_rows = [mask_pair[:, 0, :], mask_pair[:, 1, :]] + [place([P, J], F32, "mask%d" % i)[:] for i in (2, 3)]
+        whole = {r: place([P, T], F32, "val%d" % r, (2 + r) * ROW) for r in (1, 2)}
+        parts = {r: [place([P, T // 2], F32, "val%d_%d" % (r, h)) for h in range(2)] for r in (0, 3)}
 
-        def load_part(r, h):
-            nc.sync.dma_start(parts[r][h][:], vals[P * r : P * (r + 1), T // 2 * h : T // 2 * (h + 1)])
-
-        def load_mask(i):
-            nc.sync.dma_start(mask_rows[i][:], mask[P * i : P * (i + 1), :])
-
-        def load_values(r):
-            nc.sync.dma_start(val_pool[r][:], vals[P * r : P * (r + 1), :])
+        def load_parts(r):
+            for h in range(2):
+                nc.sync.dma_start(parts[r][h][:], vals[P * r : P * (r + 1), T // 2 * h : T // 2 * (h + 1)])
 
         nc.vector.memset(k_byte_pool[:].bitcast(I32), 0)
         nc.vector.memset(q_byte_pool[:].bitcast(I32), 0)
         nc.sync.dma_start(k_list[:], offs2)
         nc.scalar.dma_start(size_cols[:], size[0].rearrange("(n m) -> n m", m=4))
         load_words(k_word_pool, keys_words)
-        load_scales(nc.sync, k_byte_pool, keys_scales, 0)
+        load_scales(k_byte_pool, keys_scales, 0)
         nc.sync.dma_start(q_list[:], offs)
         load_words(q_word_pool, qpool_words)
-        load_scales(nc.sync, q_byte_pool, qpool_scales, 4)
-        load_part(0, 0)
-        load_mask(0)
-        load_mask(1)
-        load_part(0, 1)
-        load_mask(2)
-        load_mask(3)
-        load_values(1)
-        load_values(2)
-        load_part(3, 0)
-        load_part(3, 1)
+        load_scales(q_byte_pool, qpool_scales, 4)
+        nc.sync.dma_start(mask_pair[:], mask[0 : 2 * P, :].rearrange("(n p) j -> p n j", p=P))
+        load_parts(0)
+        for i in (2, 3):
+            nc.sync.dma_start(mask_rows[i], mask[P * i : P * (i + 1), :])
+        for r in (1, 2):
+            nc.sync.dma_start(whole[r][:], vals[P * r : P * (r + 1), :])
+        load_parts(3)
 
-        windows = [keep.tile([P, T], F32, name="window%d" % b) for b in range(3)]
-        ident = keep.tile([P, P], F32, name="ident")
+        windows = [place([P, T], F32, "window%d" % b) for b in range(2)]
+        ident = place([P, P], F32, "ident")
         make_identity(nc, ident[:])
         for window in windows:
             nc.vector.memset(window[:].bitcast(I32), 0)
 
-        size_all = psum.tile([P, 4, P], F32, name="size_all", tag="bank7")
+        size_all = bank([P, 4, P], "size_all", 7)
         for m in range(4):
             nc.tensor.transpose(size_all[:, m, :], size_cols[:, m : m + 1].to_broadcast([P, P]), ident[:])
-        size_rows = keep.tile([P, J], F32, name="size_rows")
-        nc.scalar.copy(size_rows[:].rearrange("p (n m) -> p n m", m=4), size_all[:].rearrange("p m n -> p n m"))
+        size_rows = size_all[:].rearrange("p m n -> p n m")
 
-        k_words = keep.tile([P, J], U32, name="k_words", align_bytes=64)
-        k_bytes = keep.tile([P, J], U8, name="k_bytes", align_bytes=64)
-        q_bytes = keep.tile([P, I], U8, name="q_bytes", align_bytes=64)
+        k_words = place([P, J], U32, "k_words")
+        k_bytes = place([P, J], U8, "k_bytes")
+        q_bytes = place([P, I], U8, "q_bytes")
         nc.vector.tensor_copy(k_words[:], k_word_pool[:].bitcast(U32).indirect(k_list[:]))
         nc.vector.tensor_copy(k_bytes[:], k_byte_pool[:].indirect(k_list[:]))
         scores = []
 
-        def gather_query_words(half, tag):
-            words = keep.tile([P, HALF], U32, name="q_words%d" % half, tag=tag, align_bytes=64)
-            nc.vector.tensor_copy(words[:], q_word_pool[:].bitcast(U32).indirect(q_list[:, 16 * half : 16 * (half + 1)]))
+        def q_half(half):
+            return q_list[:, 16 * half : 16 * (half + 1)]
+
+        def gather_query_words(half, where):
+            words = place([P, HALF], U32, "q_words%d" % half, where)
+            nc.vector.tensor_copy(words[:], q_word_pool[:].bitcast(U32).indirect(q_half(half)))
             return words
 
         def gather_query_bytes(half):
-            nc.vector.tensor_copy(
-                q_bytes[:, HALF * half : HALF * (half + 1)],
-                q_byte_pool[:].indirect(q_list[:, 16 * half : 16 * (half + 1)]),
+            nc.vector.tensor_copy(q_bytes[:, HALF * half : HALF * (half + 1)], q_byte_pool[:].indirect(q_half(half)))
+
+        def multiply(result, lhs, lhs_scale, rhs, rhs_scale):
+            nc.tensor.matmul_mx(
+                out=result, lhsT=lhs.bitcast(FP8X4), lhsT_scale=lhs_scale, rhs=rhs.bitcast(FP8X4), rhs_scale=rhs_scale, start=True, stop=True
             )
 
         def score(half, words):
             for n in range(2):
                 i = 2 * half + n
-                bank = psum.tile([P, J], F32, name="score%d" % i, tag="bank%d" % i)
-                nc.tensor.matmul_mx(
-                    out=bank[:],
-                    lhsT=words[:, P * n : P * (n + 1)].bitcast(FP8X4),
-                    lhsT_scale=q_bytes[4:P, P * i : P * (i + 1)],
-                    rhs=k_words[:].bitcast(FP8X4),
-                    rhs_scale=k_bytes[:],
-                    start=True,
-                    stop=True,
-                )
-                scores.append(bank)
+                scores.append(bank([P, J], "score%d" % i, i))
+                multiply(scores[i][:], words[:, P * n : P * (n + 1)], q_bytes[4:P, P * i : P * (i + 1)], k_words[:], k_bytes[:])
 
-        first_words = gather_query_words(0, "q_words0")
+        first_words = gather_query_words(0, None)
         gather_query_bytes(0)
         score(0, first_words)
         gather_query_bytes(1)
         score(1, gather_query_words(1, "q_byte_pool"))
+        third_window = place([P, T], F32, "third_window", ROW)
+        nc.gpsimd.memset(third_window[:].bitcast(I32), 0)
 
-        def turn_pairs(rows, grouped_words, bank):
+        def turn_pairs(rows, grouped_words, number):
             words = rows[:].bitcast(F32)
-            turned = psum.tile([P, 2, P], F32, name="turned", tag="bank%d" % bank)
+            turned = bank([P, 2, P], "turned", number)
             for u in range(2):
                 nc.tensor.transpose(turned[:, u, :], words[:, u : 2 * P : 2], ident[:])
             nc.scalar.copy(grouped_words.rearrange("p (c u) -> p c u", u=2), turned[:].rearrange("p u c -> p c u"))
 
-        def round_values(r, parts):
-            rounded = keep.tile([P, T], BF16, name="rounded%d" % r)
-            width = T // len(parts)
+        def round_values(r):
+            rounded = place([P, T], BF16, "rounded%d" % r)
             for c in range(0, T, CAST):
-                nc.scalar.activation(rounded[:, c : c + CAST], parts[c // width][:, c % width : c % width + CAST], ACT.Copy)
+                part, start = divmod(c, T // 2)
+                nc.scalar.activation(rounded[:, c : c + CAST], parts[r][part][:, start : start + CAST], ACT.Copy)
             return rounded
 
-        def gather_on_scalar(r, rounded, tag):
-            picked = place([P, J], BF16, "picked%d" % r, tag)
+        def gather_on_scalar(r, rounded, where):
+            picked = place([P, J], BF16, "picked%d" % r, where)
             nc.scalar.activation(picked[:], rounded[:].indirect(k_list[:]), ACT.Copy)
             return picked
 
-        def gather_half_on_scalar(picked, rounded, half):
-            nc.scalar.activation(
-                picked[:, HALF * half : HALF * (half + 1)], rounded[:].indirect(k_list[:, 16 * half : 16 * (half + 1)]), ACT.Copy
-            )
-
-        def gather_on_vector(r, tag):
-            picked = place([P, J], BF16, "picked%d" % r, tag)
-            nc.vector.tensor_copy(picked[:], val_pool[r][:].indirect(k_list[:]))
+        def gather_on_vector(r, where):
+            picked = place([P, J], BF16, "picked%d" % r, where)
+            nc.vector.tensor_copy(picked[:], whole[r][:].indirect(k_list[:]))
             return picked
 
-        def quantize_values(r, picked, bank, grouped_tag, tag):
-            grouped = place([P, 4 * P], BF16, "v_grouped%d" % r, grouped_tag)
-            turn_pairs(picked, grouped[:].bitcast(F32), bank)
-            codes = place([P, P], U32, "v_codes%d" % r, tag)
-            scales = keep.tile([P, P], U8, name="v_scales%d" % r, align_bytes=64)
+        def turn_values(r, picked, number, where=None):
+            grouped = place([P, 4 * P], BF16, "v_grouped%d" % r, where)
+            turn_pairs(picked, grouped[:].bitcast(F32), number)
+            return grouped
+
+        def quantize_values(r, grouped):
+            codes = place([P, P], U32, "v_codes%d" % r)
+            scales = place([P, P], U8, "v_scales%d" % r)
             nc.vector.quantize_mx(out=codes[:].bitcast(FP8X4), scales=scales[:], in_=grouped[:])
             return codes, scales
 
-        def scatter(r, operand, halves, banks, tag, window):
-            codes, scales = operand
-            result = place([P, HALF * len(halves)], F32, "result%d_%d" % (r, halves[0]), tag)
-            for n, half in enumerate(halves):
-                bank = psum.tile([P, HALF], F32, name="product%d_%d" % (r, half), tag="bank%d" % banks[n])
-                nc.tensor.matmul_mx(
-                    out=bank[:],
-                    lhsT=codes[:].bitcast(FP8X4),
-                    lhsT_scale=scales[:],
-                    rhs=w_codes[half][:].bitcast(FP8X4),
-                    rhs_scale=w_scales[half][:],
-                    start=True,
-                    stop=True,
-                )
-                nc.scalar.copy(result[:, HALF * n : HALF * (n + 1)], bank[:])
-            nc.vector.tensor_copy(window[:].indirect(q_list[:, 16 * halves[0] : 16 * (halves[-1] + 1)]), result[:])
-            if halves[-1] == 1:
-                nc.sync.dma_start(out[P * r : P * (r + 1), :], window[:])
+        w_codes = place([P, I], U32, "w_codes")
+        w_scales = place([P, I], U8, "w_scales")
 
-        w_codes = {}
-        w_scales = {}
+        def product_of(r, operand, first, last, number, where=None):
+            codes, scales = operand
+            columns = slice(HALF * first, HALF * (last + 1))
+            width = HALF * (last + 1 - first)
+            product = bank([P, width], "product%d_%d" % (r, first), number)
+            multiply(product[:], codes[:], scales[:], w_codes[:, columns], w_scales[:, columns])
+            result = place([P, width], F32, "result%d_%d" % (r, first), where)
+            nc.scalar.copy(result[:], product[:])
+            return result
+
+        def scatter(r, result, first, last, window):
+            nc.vector.tensor_copy(window[:].indirect(q_list[:, 16 * first : 16 * (last + 1)]), result[:])
+            if last == 1:
+                nc.sync.dma_start(out[P * r : P * (r + 1), :], window[:])
 
         s = {}
         p = {}
-        neg_max = {}
         total = {}
         inverse = {}
+        w_grouped = [place([P, 2 * I], BF16, "w_grouped%d" % h) for h in range(2)]
 
-        def add_mask(i, tag):
-            s[i] = place([P, J], F32, "s%d" % i, tag)
-            nc.vector.tensor_tensor(s[i][:], scores[i][:], mask_rows[i][:], ALU.add)
+        def add_mask(i):
+            s[i] = place([P, J], F32, "s%d" % i)
+            nc.vector.tensor_tensor(s[i][:], scores[i][:], mask_rows[i], ALU.add)
 
-        def exponentiate(i, tag, p_tag):
-            neg_max[i] = place([P, 1], F32, "neg_max%d" % i, tag)
-            p[i] = place([P, J], F32, "p%d" % i, p_tag)
-            total[i] = keep.tile([P, 1], F32, name="total%d" % i, tag="total%d" % i, align_bytes=64)
-            nc.vector.tensor_reduce(neg_max[i][:], s[i][:], mybir.AxisListType.X, ALU.max, negate=True)
-            nc.scalar.activation(p[i][:], s[i][:], ACT.Exp, bias=neg_max[i][:], accum_out=total[i][:])
+        def exponentiate(i, where=None):
+            neg_max = place([P, 1], F32, "neg_max%d" % i)
+            total[i] = place([P, 1], F32, "total%d" % i)
+            p[i] = place([P, J], F32, "p%d" % i, where)
+            nc.vector.tensor_reduce(neg_max[:], s[i][:], mybir.AxisListType.X, ALU.max, negate=True)
+            nc.scalar.activation(p[i][:], s[i][:], ACT.Exp, bias=neg_max[:], accum_out=total[i][:])
 
-        def invert(i, tag):
-            inverse[i] = place([P, 1], F32, "inverse%d" % i, tag)
+        def invert(i):
+            inverse[i] = place([P, 1], F32, "inverse%d" % i)
             nc.vector.reciprocal(inverse[i][:], total[i][:])
 
-        def weigh(i, w_grouped, tag):
-            w = place([P, J], BF16, "w%d" % i, tag)
-            nc.vector.scalar_tensor_tensor(w[:], p[i][:], inverse[i][:], size_rows[:], ALU.mult, ALU.mult)
-            turn_pairs(w, w_grouped[:].bitcast(F32)[:, 2 * P * (i % 2) : 2 * P * (i % 2 + 1)], 4 + i % 3)
+        def weigh(i, number):
+            w = place([P, J], BF16, "w%d" % i)
+            nc.vector.scalar_tensor_tensor(
+                w[:].rearrange("p (n m) -> p n m", m=4),
+                p[i][:].rearrange("p (n m) -> p n m", m=4),
+                inverse[i][:],
+                size_rows,
+                ALU.mult,
+                ALU.mult,
+            )
+            turn_pairs(w, w_grouped[i // 2][:].bitcast(F32)[:, 2 * P * (i % 2) : 2 * P * (i % 2 + 1)], number)
 
-        def quantize_weights(half, w_grouped, tag):
-            w_codes[half] = place([P, HALF], U32, "w_codes%d" % half, tag)
-            w_scales[half] = keep.tile([P, HALF], U8, name="w_scales%d" % half, align_bytes=64)
-            nc.vector.quantize_mx(out=w_codes[half][:].bitcast(FP8X4), scales=w_scales[half][:], in_=w_grouped[:])
+        def quantize_weights(h):
+            columns = slice(HALF * h, HALF * (h + 1))
+            nc.vector.quantize_mx(out=w_codes[:, columns].bitcast(FP8X4), scales=w_scales[:, columns], in_=w_grouped[h][:])
 
-        w_first = keep.tile([P, 2 * I], BF16, name="w_first", align_bytes=64)
-        w_second = keep.tile([P, 2 * I], BF16, name="w_second", tag="w_second", align_bytes=64)
-        last_window = staged.tile([P, T], F32, name="last_window", offset=ROW)
-        nc.gpsimd.memset(last_window[:].bitcast(I32), 0)
-        add_mask(0, "s0")
-        add_mask(1, "s1")
-        exponentiate(0, "m0", "p0")
-        exponentiate(1, "m1", "p1")
-        add_mask(2, "s2")
-        add_mask(3, "s3")
-        invert(0, "i0")
-        exponentiate(2, "m2", "p2")
-        weigh(0, w_first, "w0")
-        invert(1, "i1")
-        exponentiate(3, "m3", "p3")
-        weigh(1, w_first, "w1")
-        picked1 = gather_on_vector(1, "p0")
-        invert(2, "i2")
-        v0 = quantize_values(0, gather_on_scalar(0, round_values(0, parts[0]), "s1"), 0, "g0", "v_codes0")
-        weigh(2, w_second, 4 * ROW)
-        invert(3, 4 * ROW + 1024)
-        quantize_weights(0, w_first, 4 * ROW + 2048)
-        weigh(3, w_second, "w3")
-        v1 = quantize_values(1, picked1, 1, "g1", "v_codes1")
-        picked2 = gather_on_vector(2, "p2")
-        scatter(0, v0, [0], [0], "w2x", windows[0])
-        quantize_weights(1, w_second, 5 * ROW)
-        scatter(1, v1, [0], [5], "result0", windows[1])
-        rounded3 = round_values(3, parts[3])
-        v2 = quantize_values(2, picked2, 2, 6 * ROW, "v_codes2")
-        scatter(0, v0, [1], [1], 6 * ROW + ROW // 2, windows[0])
-        scatter(1, v1, [1], [1], "result3", windows[1])
-        v3 = quantize_values(3, gather_on_scalar(3, rounded3, "picked3"), 3, "g3", "v_codes3")
-        scatter(2, v2, [0, 1], [2, 0], "picked3", windows[2])
-        scatter(3, v3, [0, 1], [5, 6], "result6", last_window)
+        rounded0 = round_values(0)
+        add_mask(0)
+        add_mask(1)
+        exponentiate(0, "val0_1")
+        exponentiate(1)
+        picked0 = gather_on_scalar(0, rounded0, None)
+        add_mask(2)
+        add_mask(3)
+        invert(0)
+        exponentiate(2)
+        exponentiate(3)
+        grouped0 = turn_values(0, picked0, 6)
+        invert(1)
+        weigh(0, 4)
+        weigh(1, 5)
+        grouped1 = turn_values(1, gather_on_vector(1, None), 0)
+        invert(2)
+        invert(3)
+        v0 = quantize_values(0, grouped0)
+        weigh(2, 1)
+        quantize_weights(0)
+        weigh(3, 2)
+        v1 = quantize_values(1, grouped1)
+        result = product_of(0, v0, 0, 0, 6)
+        grouped2 = turn_values(2, gather_on_vector(2, None), 6)
+        scatter(0, result, 0, 0, windows[0])
+        quantize_weights(1)
+        v2 = quantize_values(2, grouped2)
+        scatter(1, product_of(1, v1, 0, 0, 4), 0, 0, windows[1])
+        scatter(0, product_of(0, v0, 1, 1, 5), 1, 1, windows[0])
+        scatter(1, product_of(1, v1, 1, 1, 0), 1, 1, windows[1])
+        scatter(2, product_of(2, v2, 0, 0, 1), 0, 0, third_window)
+        v3 = quantize_values(3, turn_values(3, gather_on_scalar(3, round_values(3), None), 2))
+        scatter(2, product_of(2, v2, 1, 1, 3, "picked3"), 1, 1, third_window)
+        scatter(3, product_of(3, v3, 0, 1, 4), 0, 1, windows[0])

@@ -52,14 +52,15 @@ def tile_attend_pickboth_kernel(tc, qpool_words, qpool_scales, keys_words, keys_
         size_cols = place([P, 4], F32, "size_cols")
         k_word_pool = place([P, T], I32, "k_word_pool", 0)
         q_word_pool = place([P, T], I32, "q_word_pool", ROW)
-        mask_pair = place([P, 2, J], F32, "mask_pair")
-        mask_rows = [mask_pair[:, 0, :], mask_pair[:, 1, :]] + [place([P, J], F32, "mask%d" % i)[:] for i in (2, 3)]
+        mask_rows = [place([P, J], F32, "mask%d" % i) for i in range(4)]
         whole = {r: place([P, T], F32, "val%d" % r, (2 + r) * ROW) for r in (1, 2)}
         parts = {r: [place([P, T // 2], F32, "val%d_%d" % (r, h)) for h in range(2)] for r in (0, 3)}
 
-        def load_parts(r):
-            for h in range(2):
-                nc.sync.dma_start(parts[r][h][:], vals[P * r : P * (r + 1), T // 2 * h : T // 2 * (h + 1)])
+        def load_part(r, h):
+            nc.sync.dma_start(parts[r][h][:], vals[P * r : P * (r + 1), T // 2 * h : T // 2 * (h + 1)])
+
+        def load_mask(i):
+            nc.sync.dma_start(mask_rows[i][:], mask[P * i : P * (i + 1), :])
 
         nc.vector.memset(k_byte_pool[:].bitcast(I32), 0)
         nc.vector.memset(q_byte_pool[:].bitcast(I32), 0)
@@ -70,13 +71,16 @@ def tile_attend_pickboth_kernel(tc, qpool_words, qpool_scales, keys_words, keys_
         nc.sync.dma_start(q_list[:], offs)
         load_words(q_word_pool, qpool_words)
         load_scales(q_byte_pool, qpool_scales, 4)
-        nc.sync.dma_start(mask_pair[:], mask[0 : 2 * P, :].rearrange("(n p) j -> p n j", p=P))
-        load_parts(0)
-        for i in (2, 3):
-            nc.sync.dma_start(mask_rows[i], mask[P * i : P * (i + 1), :])
+        load_part(0, 0)
+        load_mask(0)
+        load_mask(1)
+        load_part(0, 1)
+        load_mask(2)
+        load_mask(3)
         for r in (1, 2):
             nc.sync.dma_start(whole[r][:], vals[P * r : P * (r + 1), :])
-        load_parts(3)
+        load_part(3, 0)
+        load_part(3, 1)
 
         windows = [place([P, T], F32, "window%d" % b) for b in range(2)]
         ident = place([P, P], F32, "ident")
@@ -87,7 +91,8 @@ def tile_attend_pickboth_kernel(tc, qpool_words, qpool_scales, keys_words, keys_
         size_all = bank([P, 4, P], "size_all", 7)
         for m in range(4):
             nc.tensor.transpose(size_all[:, m, :], size_cols[:, m : m + 1].to_broadcast([P, P]), ident[:])
-        size_rows = size_all[:].rearrange("p m n -> p n m")
+        size_rows = place([P, J], F32, "size_rows")
+        nc.scalar.copy(size_rows[:].rearrange("p (n m) -> p n m", m=4), size_all[:].rearrange("p m n -> p n m"))
 
         k_words = place([P, J], U32, "k_words")
         k_bytes = place([P, J], U8, "k_bytes")
@@ -133,16 +138,16 @@ def tile_attend_pickboth_kernel(tc, qpool_words, qpool_scales, keys_words, keys_
                 nc.tensor.transpose(turned[:, u, :], words[:, u : 2 * P : 2], ident[:])
             nc.scalar.copy(grouped_words.rearrange("p (c u) -> p c u", u=2), turned[:].rearrange("p u c -> p c u"))
 
-        def round_values(r):
-            rounded = place([P, T], BF16, "rounded%d" % r)
-            for c in range(0, T, CAST):
-                part, start = divmod(c, T // 2)
-                nc.scalar.activation(rounded[:, c : c + CAST], parts[r][part][:, start : start + CAST], ACT.Copy)
-            return rounded
+        rounded = {r: place([P, T], BF16, "rounded%d" % r) for r in parts}
 
-        def gather_on_scalar(r, rounded, where):
+        def round_part(r, h):
+            for c in range(0, T // 2, CAST):
+                first = T // 2 * h + c
+                nc.scalar.activation(rounded[r][:, first : first + CAST], parts[r][h][:, c : c + CAST], ACT.Copy)
+
+        def gather_on_scalar(r, where):
             picked = place([P, J], BF16, "picked%d" % r, where)
-            nc.scalar.activation(picked[:], rounded[:].indirect(k_list[:]), ACT.Copy)
+            nc.scalar.activation(picked[:], rounded[r][:].indirect(k_list[:]), ACT.Copy)
             return picked
 
         def gather_on_vector(r, where):
@@ -155,8 +160,8 @@ def tile_attend_pickboth_kernel(tc, qpool_words, qpool_scales, keys_words, keys_
             turn_pairs(picked, grouped[:].bitcast(F32), number)
             return grouped
 
-        def quantize_values(r, grouped):
-            codes = place([P, P], U32, "v_codes%d" % r)
+        def quantize_values(r, grouped, where=None):
+            codes = place([P, P], U32, "v_codes%d" % r, where)
             scales = place([P, P], U8, "v_scales%d" % r)
             nc.vector.quantize_mx(out=codes[:].bitcast(FP8X4), scales=scales[:], in_=grouped[:])
             return codes, scales
@@ -187,7 +192,7 @@ def tile_attend_pickboth_kernel(tc, qpool_words, qpool_scales, keys_words, keys_
 
         def add_mask(i):
             s[i] = place([P, J], F32, "s%d" % i)
-            nc.vector.tensor_tensor(s[i][:], scores[i][:], mask_rows[i], ALU.add)
+            nc.vector.tensor_tensor(s[i][:], scores[i][:], mask_rows[i][:], ALU.add)
 
         def exponentiate(i, where=None):
             neg_max = place([P, 1], F32, "neg_max%d" % i)
@@ -200,54 +205,52 @@ def tile_attend_pickboth_kernel(tc, qpool_words, qpool_scales, keys_words, keys_
             inverse[i] = place([P, 1], F32, "inverse%d" % i)
             nc.vector.reciprocal(inverse[i][:], total[i][:])
 
-        def weigh(i, number):
-            w = place([P, J], BF16, "w%d" % i)
-            nc.vector.scalar_tensor_tensor(
-                w[:].rearrange("p (n m) -> p n m", m=4),
-                p[i][:].rearrange("p (n m) -> p n m", m=4),
-                inverse[i][:],
-                size_rows,
-                ALU.mult,
-                ALU.mult,
-            )
+        def weigh(i, number, where=None):
+            w = place([P, J], BF16, "w%d" % i, where)
+            nc.vector.scalar_tensor_tensor(w[:], p[i][:], inverse[i][:], size_rows[:], ALU.mult, ALU.mult)
             turn_pairs(w, w_grouped[i // 2][:].bitcast(F32)[:, 2 * P * (i % 2) : 2 * P * (i % 2 + 1)], number)
 
         def quantize_weights(h):
             columns = slice(HALF * h, HALF * (h + 1))
             nc.vector.quantize_mx(out=w_codes[:, columns].bitcast(FP8X4), scales=w_scales[:, columns], in_=w_grouped[h][:])
 
-        rounded0 = round_values(0)
+        round_part(0, 0)
         add_mask(0)
         add_mask(1)
-        exponentiate(0, "val0_1")
+        exponentiate(0)
         exponentiate(1)
-        picked0 = gather_on_scalar(0, rounded0, None)
+        round_part(0, 1)
         add_mask(2)
         add_mask(3)
         invert(0)
         exponentiate(2)
         exponentiate(3)
-        grouped0 = turn_values(0, picked0, 6)
+        picked0 = gather_on_scalar(0, "s3")
         invert(1)
         weigh(0, 4)
         weigh(1, 5)
-        grouped1 = turn_values(1, gather_on_vector(1, None), 0)
+        grouped0 = turn_values(0, picked0, 6)
         invert(2)
+        grouped1 = turn_values(1, gather_on_vector(1, None), 0)
         invert(3)
-        v0 = quantize_values(0, grouped0)
-        weigh(2, 1)
+        weigh(2, 1, 3 * ROW)
+        weigh(3, 2, 3 * ROW + 2 * J)
         quantize_weights(0)
-        weigh(3, 2)
+        v0 = quantize_values(0, grouped0)
         v1 = quantize_values(1, grouped1)
-        result = product_of(0, v0, 0, 0, 6)
-        grouped2 = turn_values(2, gather_on_vector(2, None), 6)
-        scatter(0, result, 0, 0, windows[0])
+        result = product_of(0, v0, 0, 0, 7)
+        picked2 = gather_on_vector(2, None)
+        grouped2 = turn_values(2, picked2, 7)
         quantize_weights(1)
+        scatter(0, result, 0, 0, windows[0])
         v2 = quantize_values(2, grouped2)
         scatter(1, product_of(1, v1, 0, 0, 4), 0, 0, windows[1])
-        scatter(0, product_of(0, v0, 1, 1, 5), 1, 1, windows[0])
-        scatter(1, product_of(1, v1, 1, 1, 0), 1, 1, windows[1])
-        scatter(2, product_of(2, v2, 0, 0, 1), 0, 0, third_window)
-        v3 = quantize_values(3, turn_values(3, gather_on_scalar(3, round_values(3), None), 2))
+        round_part(3, 0)
+        scatter(0, product_of(0, v0, 1, 1, 5, "val3_0"), 1, 1, windows[0])
+        round_part(3, 1)
+        scatter(1, product_of(1, v1, 1, 1, 0, "val3_1"), 1, 1, windows[1])
+        picked3 = gather_on_scalar(3, None)
+        scatter(2, product_of(2, v2, 0, 0, 1, "rounded3"), 0, 0, third_window)
+        v3 = quantize_values(3, turn_values(3, picked3, 2))
         scatter(2, product_of(2, v2, 1, 1, 3, "picked3"), 1, 1, third_window)
         scatter(3, product_of(3, v3, 0, 1, 4), 0, 1, windows[0])

@@ -62,15 +62,15 @@ def tile_attend_pickboth_kernel(tc, qpool_words, qpool_scales, keys_words, keys_
         def load_mask(i):
             nc.sync.dma_start(mask_rows[i][:], mask[P * i : P * (i + 1), :])
 
-        nc.vector.memset(k_byte_pool[:].bitcast(I32), 0)
+        nc.gpsimd.memset(k_byte_pool[:].bitcast(I32), 0)
         nc.vector.memset(q_byte_pool[:].bitcast(I32), 0)
         nc.sync.dma_start(k_list[:], offs2)
-        nc.scalar.dma_start(size_cols[:], size[0].rearrange("(n m) -> n m", m=4))
-        load_words(k_word_pool, keys_words)
-        load_scales(k_byte_pool, keys_scales, 0)
         nc.sync.dma_start(q_list[:], offs)
-        load_words(q_word_pool, qpool_words)
+        nc.sync.dma_start(size_cols[:], size[0].rearrange("(n m) -> n m", m=4))
+        load_scales(k_byte_pool, keys_scales, 0)
+        load_words(k_word_pool, keys_words)
         load_scales(q_byte_pool, qpool_scales, 4)
+        load_words(q_word_pool, qpool_words)
         load_part(0, 0)
         load_mask(0)
         load_mask(1)
@@ -82,11 +82,10 @@ def tile_attend_pickboth_kernel(tc, qpool_words, qpool_scales, keys_words, keys_
         load_part(3, 0)
         load_part(3, 1)
 
-        windows = [place([P, T], F32, "window%d" % b) for b in range(2)]
+        windows = [place([P, T], F32, "window0")]
         ident = place([P, P], F32, "ident")
         make_identity(nc, ident[:])
-        for window in windows:
-            nc.vector.memset(window[:].bitcast(I32), 0)
+        nc.vector.memset(windows[0][:].bitcast(I32), 0)
 
         size_all = bank([P, 4, P], "size_all", 7)
         for m in range(4):
@@ -97,8 +96,9 @@ def tile_attend_pickboth_kernel(tc, qpool_words, qpool_scales, keys_words, keys_
         k_words = place([P, J], U32, "k_words")
         k_bytes = place([P, J], U8, "k_bytes")
         q_bytes = place([P, I], U8, "q_bytes")
-        nc.vector.tensor_copy(k_words[:], k_word_pool[:].bitcast(U32).indirect(k_list[:]))
         nc.vector.tensor_copy(k_bytes[:], k_byte_pool[:].indirect(k_list[:]))
+        nc.vector.tensor_copy(k_words[:], k_word_pool[:].bitcast(U32).indirect(k_list[:]))
+        nc.vector.tensor_copy(q_bytes[:], q_byte_pool[:].indirect(q_list[:]))
         scores = []
 
         def q_half(half):
@@ -108,9 +108,6 @@ def tile_attend_pickboth_kernel(tc, qpool_words, qpool_scales, keys_words, keys_
             words = place([P, HALF], U32, "q_words%d" % half, where)
             nc.vector.tensor_copy(words[:], q_word_pool[:].bitcast(U32).indirect(q_half(half)))
             return words
-
-        def gather_query_bytes(half):
-            nc.vector.tensor_copy(q_bytes[:, HALF * half : HALF * (half + 1)], q_byte_pool[:].indirect(q_half(half)))
 
         def multiply(result, lhs, lhs_scale, rhs, rhs_scale):
             nc.tensor.matmul_mx(
@@ -123,12 +120,11 @@ def tile_attend_pickboth_kernel(tc, qpool_words, qpool_scales, keys_words, keys_
                 scores.append(bank([P, J], "score%d" % i, i))
                 multiply(scores[i][:], words[:, P * n : P * (n + 1)], q_bytes[4:P, P * i : P * (i + 1)], k_words[:], k_bytes[:])
 
-        first_words = gather_query_words(0, None)
-        gather_query_bytes(0)
-        score(0, first_words)
-        gather_query_bytes(1)
-        score(1, gather_query_words(1, "q_byte_pool"))
-        third_window = place([P, T], F32, "third_window", ROW)
+        score(0, gather_query_words(0, None))
+        score(1, gather_query_words(1, None))
+        windows.append(place([P, T], F32, "window1", ROW))
+        third_window = place([P, T], F32, "third_window", "q_words1")
+        nc.gpsimd.memset(windows[1][:].bitcast(I32), 0)
         nc.gpsimd.memset(third_window[:].bitcast(I32), 0)
 
         def turn_pairs(rows, grouped_words, number):

@@ -52,15 +52,17 @@ def tile_attend_pickboth_kernel(tc, qpool_words, qpool_scales, keys_words, keys_
         size_cols = place([P, 4], F32, "size_cols")
         k_word_pool = place([P, T], I32, "k_word_pool", 0)
         q_word_pool = place([P, T], I32, "q_word_pool", ROW)
-        mask_rows = [place([P, J], F32, "mask%d" % i) for i in range(4)]
+        mask_pair = place([P, 2, J], F32, "mask_pair")
+        mask_rows = [mask_pair[:, 0, :], mask_pair[:, 1, :]] + [place([P, J], F32, "mask%d" % i)[:] for i in (2, 3)]
         whole = {r: place([P, T], F32, "val%d" % r, (2 + r) * ROW) for r in (1, 2)}
-        parts = {r: [place([P, T // 2], F32, "val%d_%d" % (r, h)) for h in range(2)] for r in (0, 3)}
+        widths = {0: T // 4, 3: T // 2}
+        parts = {r: [place([P, w], F32, "val%d_%d" % (r, h)) for h in range(T // w)] for r, w in widths.items()}
 
         def load_part(r, h):
-            nc.sync.dma_start(parts[r][h][:], vals[P * r : P * (r + 1), T // 2 * h : T // 2 * (h + 1)])
+            nc.sync.dma_start(parts[r][h][:], vals[P * r : P * (r + 1), widths[r] * h : widths[r] * (h + 1)])
 
         def load_mask(i):
-            nc.sync.dma_start(mask_rows[i][:], mask[P * i : P * (i + 1), :])
+            nc.sync.dma_start(mask_rows[i], mask[P * i : P * (i + 1), :])
 
         nc.gpsimd.memset(k_byte_pool[:].bitcast(I32), 0)
         nc.vector.memset(q_byte_pool[:].bitcast(I32), 0)
@@ -71,12 +73,12 @@ def tile_attend_pickboth_kernel(tc, qpool_words, qpool_scales, keys_words, keys_
         load_words(k_word_pool, keys_words)
         load_scales(q_byte_pool, qpool_scales, 4)
         load_words(q_word_pool, qpool_words)
-        load_part(0, 0)
-        load_mask(0)
-        load_mask(1)
-        load_part(0, 1)
+        nc.sync.dma_start(mask_pair[:], mask[0 : 2 * P, :].rearrange("(n p) j -> p n j", p=P))
+        for h in range(3):
+            load_part(0, h)
         load_mask(2)
         load_mask(3)
+        load_part(0, 3)
         for r in (1, 2):
             nc.sync.dma_start(whole[r][:], vals[P * r : P * (r + 1), :])
         load_part(3, 0)
@@ -91,7 +93,9 @@ def tile_attend_pickboth_kernel(tc, qpool_words, qpool_scales, keys_words, keys_
         for m in range(4):
             nc.tensor.transpose(size_all[:, m, :], size_cols[:, m : m + 1].to_broadcast([P, P]), ident[:])
         size_rows = place([P, J], F32, "size_rows")
-        nc.scalar.copy(size_rows[:].rearrange("p (n m) -> p n m", m=4), size_all[:].rearrange("p m n -> p n m"))
+        nc.scalar.copy(
+            size_rows[:].rearrange("p (u n e) -> p u n e", u=2, e=2), size_all[:].rearrange("p (u e) n -> p u n e", e=2)
+        )
 
         k_words = place([P, J], U32, "k_words")
         k_bytes = place([P, J], U8, "k_bytes")
@@ -127,18 +131,17 @@ def tile_attend_pickboth_kernel(tc, qpool_words, qpool_scales, keys_words, keys_
         nc.gpsimd.memset(windows[1][:].bitcast(I32), 0)
         nc.gpsimd.memset(third_window[:].bitcast(I32), 0)
 
-        def turn_pairs(rows, grouped_words, number):
-            words = rows[:].bitcast(F32)
+        def turn_pairs(halves, grouped_words, number):
             turned = bank([P, 2, P], "turned", number)
             for u in range(2):
-                nc.tensor.transpose(turned[:, u, :], words[:, u : 2 * P : 2], ident[:])
+                nc.tensor.transpose(turned[:, u, :], halves[u], ident[:])
             nc.scalar.copy(grouped_words.rearrange("p (c u) -> p c u", u=2), turned[:].rearrange("p u c -> p c u"))
 
         rounded = {r: place([P, T], BF16, "rounded%d" % r) for r in parts}
 
         def round_part(r, h):
-            for c in range(0, T // 2, CAST):
-                first = T // 2 * h + c
+            for c in range(0, widths[r], CAST):
+                first = widths[r] * h + c
                 nc.scalar.activation(rounded[r][:, first : first + CAST], parts[r][h][:, c : c + CAST], ACT.Copy)
 
         def gather_on_scalar(r, where):
@@ -153,7 +156,8 @@ def tile_attend_pickboth_kernel(tc, qpool_words, qpool_scales, keys_words, keys_
 
         def turn_values(r, picked, number, where=None):
             grouped = place([P, 4 * P], BF16, "v_grouped%d" % r, where)
-            turn_pairs(picked, grouped[:].bitcast(F32), number)
+            words = picked[:].bitcast(F32)
+            turn_pairs([words[:, u : 2 * P : 2] for u in range(2)], grouped[:].bitcast(F32), number)
             return grouped
 
         def quantize_values(r, grouped, where=None):
@@ -188,14 +192,20 @@ def tile_attend_pickboth_kernel(tc, qpool_words, qpool_scales, keys_words, keys_
 
         def add_mask(i):
             s[i] = place([P, J], F32, "s%d" % i)
-            nc.vector.tensor_tensor(s[i][:], scores[i][:], mask_rows[i][:], ALU.add)
+            nc.vector.tensor_tensor(s[i][:], scores[i][:], mask_rows[i], ALU.add)
 
         def exponentiate(i, where=None):
             neg_max = place([P, 1], F32, "neg_max%d" % i)
             total[i] = place([P, 1], F32, "total%d" % i)
             p[i] = place([P, J], F32, "p%d" % i, where)
             nc.vector.tensor_reduce(neg_max[:], s[i][:], mybir.AxisListType.X, ALU.max, negate=True)
-            nc.scalar.activation(p[i][:], s[i][:], ACT.Exp, bias=neg_max[:], accum_out=total[i][:])
+            nc.scalar.activation(
+                p[i][:].rearrange("p (u n e) -> p u n e", u=2, e=2),
+                s[i][:].rearrange("p (n u e) -> p u n e", u=2, e=2),
+                ACT.Exp,
+                bias=neg_max[:],
+                accum_out=total[i][:],
+            )
 
         def invert(i):
             inverse[i] = place([P, 1], F32, "inverse%d" % i)
@@ -204,18 +214,20 @@ def tile_attend_pickboth_kernel(tc, qpool_words, qpool_scales, keys_words, keys_
         def weigh(i, number, where=None):
             w = place([P, J], BF16, "w%d" % i, where)
             nc.vector.scalar_tensor_tensor(w[:], p[i][:], inverse[i][:], size_rows[:], ALU.mult, ALU.mult)
-            turn_pairs(w, w_grouped[i // 2][:].bitcast(F32)[:, 2 * P * (i % 2) : 2 * P * (i % 2 + 1)], number)
+            words = w[:].bitcast(F32)
+            turn_pairs([words[:, P * u : P * (u + 1)] for u in range(2)], w_grouped[i // 2][:].bitcast(F32)[:, 2 * P * (i % 2) : 2 * P * (i % 2 + 1)], number)
 
         def quantize_weights(h):
             columns = slice(HALF * h, HALF * (h + 1))
             nc.vector.quantize_mx(out=w_codes[:, columns].bitcast(FP8X4), scales=w_scales[:, columns], in_=w_grouped[h][:])
 
-        round_part(0, 0)
+        for h in range(3):
+            round_part(0, h)
         add_mask(0)
         add_mask(1)
         exponentiate(0)
         exponentiate(1)
-        round_part(0, 1)
+        round_part(0, 3)
         add_mask(2)
         add_mask(3)
         invert(0)

@@ -181,8 +181,11 @@ def tile_attend_pickboth_kernel(tc, qpool_words, qpool_scales, keys_words, keys_
 
         def scatter(r, result, first, last, window):
             nc.vector.tensor_copy(window[:].indirect(q_list[:, 16 * first : 16 * (last + 1)]), result[:])
-            if last == 1:
+            if last == 1 and r < 3:
                 nc.sync.dma_start(out[P * r : P * (r + 1), :], window[:])
+            elif last == 1:
+                nc.sync.dma_start(out[P * r : P * (r + 1), 0 : T // 2], window[:, 0 : T // 2])
+                nc.scalar.dma_start(out[P * r : P * (r + 1), T // 2 : T], window[:, T // 2 : T])
 
         s = {}
         p = {}

@@ -17,7 +17,6 @@ ALU = mybir.AluOpType
 ACT = mybir.ActivationFunctionType
 
 P = 128
-CAST = 512
 HALF = 256
 ROW = 4 * T
 
@@ -54,12 +53,10 @@ def tile_attend_pickboth_kernel(tc, qpool_words, qpool_scales, keys_words, keys_
         q_word_pool = place([P, T], I32, "q_word_pool", ROW)
         mask_pair = place([P, 2, J], F32, "mask_pair")
         mask_rows = [mask_pair[:, 0, :], mask_pair[:, 1, :]] + [place([P, J], F32, "mask%d" % i)[:] for i in (2, 3)]
-        whole = {r: place([P, T], F32, "val%d" % r, (2 + r) * ROW) for r in (1, 2)}
-        widths = {0: T // 4, 3: T // 2}
-        parts = {r: [place([P, w], F32, "val%d_%d" % (r, h)) for h in range(T // w)] for r, w in widths.items()}
+        val = [place([P, T], F32, "val%d" % r, (2 + r) * ROW) for r in range(4)]
 
-        def load_part(r, h):
-            nc.sync.dma_start(parts[r][h][:], vals[P * r : P * (r + 1), widths[r] * h : widths[r] * (h + 1)])
+        def load_values(r):
+            nc.sync.dma_start(val[r][:], vals[P * r : P * (r + 1), :])
 
         def load_mask(i):
             nc.sync.dma_start(mask_rows[i], mask[P * i : P * (i + 1), :])
@@ -74,20 +71,17 @@ def tile_attend_pickboth_kernel(tc, qpool_words, qpool_scales, keys_words, keys_
         load_scales(q_byte_pool, qpool_scales, 4)
         load_words(q_word_pool, qpool_words)
         nc.sync.dma_start(mask_pair[:], mask[0 : 2 * P, :].rearrange("(n p) j -> p n j", p=P))
-        for h in range(3):
-            load_part(0, h)
         load_mask(2)
         load_mask(3)
-        load_part(0, 3)
-        for r in (1, 2):
-            nc.sync.dma_start(whole[r][:], vals[P * r : P * (r + 1), :])
-        load_part(3, 0)
-        load_part(3, 1)
+        for r in range(4):
+            load_values(r)
 
-        windows = [place([P, T], F32, "window0")]
+        windows = [place([P, T], F32, "window%d" % r) for r in range(4)]
         ident = place([P, P], F32, "ident")
         make_identity(nc, ident[:])
         nc.vector.memset(windows[0][:].bitcast(I32), 0)
+        for r in (1, 2, 3):
+            nc.gpsimd.memset(windows[r][:].bitcast(I32), 0)
 
         size_all = bank([P, 4, P], "size_all", 7)
         for m in range(4):
@@ -105,31 +99,16 @@ def tile_attend_pickboth_kernel(tc, qpool_words, qpool_scales, keys_words, keys_
         nc.vector.tensor_copy(q_bytes[:], q_byte_pool[:].indirect(q_list[:]))
         scores = []
 
-        def q_half(half):
-            return q_list[:, 16 * half : 16 * (half + 1)]
-
-        def gather_query_words(half, where):
-            words = place([P, HALF], U32, "q_words%d" % half, where)
-            nc.vector.tensor_copy(words[:], q_word_pool[:].bitcast(U32).indirect(q_half(half)))
-            return words
-
         def multiply(result, lhs, lhs_scale, rhs, rhs_scale):
             nc.tensor.matmul_mx(
                 out=result, lhsT=lhs.bitcast(FP8X4), lhsT_scale=lhs_scale, rhs=rhs.bitcast(FP8X4), rhs_scale=rhs_scale, start=True, stop=True
             )
 
-        def score(half, words):
-            for n in range(2):
-                i = 2 * half + n
-                scores.append(bank([P, J], "score%d" % i, i))
-                multiply(scores[i][:], words[:, P * n : P * (n + 1)], q_bytes[4:P, P * i : P * (i + 1)], k_words[:], k_bytes[:])
-
-        score(0, gather_query_words(0, None))
-        score(1, gather_query_words(1, None))
-        windows.append(place([P, T], F32, "window1", ROW))
-        third_window = place([P, T], F32, "third_window", "q_words1")
-        nc.gpsimd.memset(windows[1][:].bitcast(I32), 0)
-        nc.gpsimd.memset(third_window[:].bitcast(I32), 0)
+        for i in range(4):
+            words = place([P, P], U32, "q_words%d" % i)
+            nc.vector.tensor_copy(words[:], q_word_pool[:].bitcast(U32).indirect(q_list[:, 8 * i : 8 * (i + 1)]))
+            scores.append(bank([P, J], "score%d" % i, i))
+            multiply(scores[i][:], words[:], q_bytes[4:P, P * i : P * (i + 1)], k_words[:], k_bytes[:])
 
         def turn_pairs(halves, grouped_words, number):
             turned = bank([P, 2, P], "turned", number)
@@ -137,21 +116,12 @@ def tile_attend_pickboth_kernel(tc, qpool_words, qpool_scales, keys_words, keys_
                 nc.tensor.transpose(turned[:, u, :], halves[u], ident[:])
             nc.scalar.copy(grouped_words.rearrange("p (c u) -> p c u", u=2), turned[:].rearrange("p u c -> p c u"))
 
-        rounded = {r: place([P, T], BF16, "rounded%d" % r) for r in parts}
-
-        def round_part(r, h):
-            for c in range(0, widths[r], CAST):
-                first = widths[r] * h + c
-                nc.scalar.activation(rounded[r][:, first : first + CAST], parts[r][h][:, c : c + CAST], ACT.Copy)
-
-        def gather_on_scalar(r, where):
+        def gather_values(r, on_scalar, where=None):
             picked = place([P, J], BF16, "picked%d" % r, where)
-            nc.scalar.activation(picked[:], rounded[r][:].indirect(k_list[:]), ACT.Copy)
-            return picked
-
-        def gather_on_vector(r, where):
-            picked = place([P, J], BF16, "picked%d" % r, where)
-            nc.vector.tensor_copy(picked[:], whole[r][:].indirect(k_list[:]))
+            if on_scalar:
+                nc.scalar.activation(picked[:], val[r][:].indirect(k_list[:]), ACT.Copy)
+            else:
+                nc.vector.tensor_copy(picked[:], val[r][:].indirect(k_list[:]))
             return picked
 
         def turn_values(r, picked, number, where=None):
@@ -169,25 +139,30 @@ def tile_attend_pickboth_kernel(tc, qpool_words, qpool_scales, keys_words, keys_
         w_codes = place([P, I], U32, "w_codes")
         w_scales = place([P, I], U8, "w_scales")
 
-        def product_of(r, operand, first, last, number, where=None):
+        def product_of(r, operand, first, last, number, on_scalar, where=None):
             codes, scales = operand
             columns = slice(HALF * first, HALF * (last + 1))
             width = HALF * (last + 1 - first)
             product = bank([P, width], "product%d_%d" % (r, first), number)
             multiply(product[:], codes[:], scales[:], w_codes[:, columns], w_scales[:, columns])
             result = place([P, width], F32, "result%d_%d" % (r, first), where)
-            nc.scalar.copy(result[:], product[:])
-            return result
+            if on_scalar:
+                nc.scalar.copy(result[:], product[:])
+            else:
+                nc.vector.tensor_copy(result[:], product[:])
+            return result[:]
 
-        def scatter(r, result, first, last, window):
-            nc.vector.tensor_copy(window[:].indirect(q_list[:, 16 * first : 16 * (last + 1)]), result[:])
-            if last == 1 and r < 3:
-                nc.sync.dma_start(out[P * r : P * (r + 1), :], window[:])
-            elif last == 1:
-                nc.sync.dma_start(out[P * r : P * (r + 1), 0 : T // 2], window[:, 0 : T // 2])
-                nc.scalar.dma_start(out[P * r : P * (r + 1), T // 2 : T], window[:, T // 2 : T])
+        def scatter(r, result, first, last, on_scalar):
+            places = windows[r][:].indirect(q_list[:, 16 * first : 16 * (last + 1)])
+            if on_scalar:
+                nc.scalar.activation(places, result, ACT.Copy)
+            else:
+                nc.vector.tensor_copy(places, result)
+            if last == 1:
+                nc.sync.dma_start(out[P * r : P * (r + 1), :], windows[r][:])
 
         s = {}
+        neg_max = {}
         p = {}
         total = {}
         inverse = {}
@@ -197,16 +172,18 @@ def tile_attend_pickboth_kernel(tc, qpool_words, qpool_scales, keys_words, keys_
             s[i] = place([P, J], F32, "s%d" % i)
             nc.vector.tensor_tensor(s[i][:], scores[i][:], mask_rows[i], ALU.add)
 
+        def find_max(i):
+            neg_max[i] = place([P, 1], F32, "neg_max%d" % i)
+            nc.vector.tensor_reduce(neg_max[i][:], s[i][:], mybir.AxisListType.X, ALU.max, negate=True)
+
         def exponentiate(i, where=None):
-            neg_max = place([P, 1], F32, "neg_max%d" % i)
             total[i] = place([P, 1], F32, "total%d" % i)
             p[i] = place([P, J], F32, "p%d" % i, where)
-            nc.vector.tensor_reduce(neg_max[:], s[i][:], mybir.AxisListType.X, ALU.max, negate=True)
             nc.scalar.activation(
                 p[i][:].rearrange("p (u n e) -> p u n e", u=2, e=2),
                 s[i][:].rearrange("p (n u e) -> p u n e", u=2, e=2),
                 ACT.Exp,
-                bias=neg_max[:],
+                bias=neg_max[i][:],
                 accum_out=total[i][:],
             )
 
@@ -224,44 +201,51 @@ def tile_attend_pickboth_kernel(tc, qpool_words, qpool_scales, keys_words, keys_
             columns = slice(HALF * h, HALF * (h + 1))
             nc.vector.quantize_mx(out=w_codes[:, columns].bitcast(FP8X4), scales=w_scales[:, columns], in_=w_grouped[h][:])
 
-        for h in range(3):
-            round_part(0, h)
+        spare = 6 * ROW
         add_mask(0)
         add_mask(1)
+        find_max(0)
+        find_max(1)
         exponentiate(0)
         exponentiate(1)
-        round_part(0, 3)
+        picked0 = gather_values(0, True)
         add_mask(2)
         add_mask(3)
         invert(0)
-        exponentiate(2)
-        exponentiate(3)
-        picked0 = gather_on_scalar(0, "s3")
+        find_max(2)
         invert(1)
+        find_max(3)
+        exponentiate(2, 2 * ROW)
+        exponentiate(3)
+        grouped0 = turn_values(0, picked0, 6, "s3")
         weigh(0, 4)
         weigh(1, 5)
-        grouped0 = turn_values(0, picked0, 6)
+        picked1 = gather_values(1, True, "w1")
         invert(2)
-        grouped1 = turn_values(1, gather_on_vector(1, None), 0)
         invert(3)
-        weigh(2, 1, 3 * ROW)
-        weigh(3, 2, 3 * ROW + 2 * J)
+        weigh(2, 7)
+        v0 = quantize_values(0, grouped0, spare)
+        weigh(3, 0)
         quantize_weights(0)
-        v0 = quantize_values(0, grouped0)
-        v1 = quantize_values(1, grouped1)
-        result = product_of(0, v0, 0, 0, 7)
-        picked2 = gather_on_vector(2, None)
-        grouped2 = turn_values(2, picked2, 7)
+        result00 = product_of(0, v0, 0, 0, 1, True, spare + 512)
+        grouped1 = turn_values(1, picked1, 7)
+        scatter(0, result00, 0, 0, True)
+        picked2 = gather_values(2, False)
         quantize_weights(1)
-        scatter(0, result, 0, 0, windows[0])
-        v2 = quantize_values(2, grouped2)
-        scatter(1, product_of(1, v1, 0, 0, 4), 0, 0, windows[1])
-        round_part(3, 0)
-        scatter(0, product_of(0, v0, 1, 1, 5, "val3_0"), 1, 1, windows[0])
-        round_part(3, 1)
-        scatter(1, product_of(1, v1, 1, 1, 0, "val3_1"), 1, 1, windows[1])
-        picked3 = gather_on_scalar(3, None)
-        scatter(2, product_of(2, v2, 0, 0, 1, "rounded3"), 0, 0, third_window)
-        v3 = quantize_values(3, turn_values(3, picked3, 2))
-        scatter(2, product_of(2, v2, 1, 1, 3, "picked3"), 1, 1, third_window)
-        scatter(3, product_of(3, v3, 0, 1, 4), 0, 1, windows[0])
+        v1 = quantize_values(1, grouped1)
+        result01 = product_of(0, v0, 1, 1, 2, True)
+        grouped2 = turn_values(2, picked2, 3, spare)
+        scatter(0, result01, 1, 1, True)
+        picked3 = gather_values(3, False)
+        result10 = product_of(1, v1, 0, 0, 4, False, 5 * ROW)
+        v2 = quantize_values(2, grouped2, 5 * ROW + 1024)
+        scatter(1, result10, 0, 0, False)
+        grouped3 = turn_values(3, picked3, 6)
+        result11 = product_of(1, v1, 1, 1, 5, True, "picked3")
+        v3 = quantize_values(3, grouped3)
+        scatter(1, result11, 1, 1, False)
+        result20 = product_of(2, v2, 0, 0, 0, True)
+        result21 = product_of(2, v2, 1, 1, 1, True)
+        scatter(2, result20, 0, 0, True)
+        scatter(2, result21, 1, 1, True)
+        scatter(3, product_of(3, v3, 0, 1, 7, False), 0, 1, False)

@@ -110,11 +110,20 @@ def tile_attend_pickboth_kernel(tc, qpool_words, qpool_scales, keys_words, keys_
             scores.append(bank([P, J], "score%d" % i, i))
             multiply(scores[i][:], words[:], q_bytes[4:P, P * i : P * (i + 1)], k_words[:], k_bytes[:])
 
-        def turn_pairs(halves, grouped_words, number):
+        def turn_pairs(halves, number):
             turned = bank([P, 2, P], "turned", number)
             for u in range(2):
                 nc.tensor.transpose(turned[:, u, :], halves[u], ident[:])
-            nc.scalar.copy(grouped_words.rearrange("p (c u) -> p c u", u=2), turned[:].rearrange("p u c -> p c u"))
+            return turned
+
+        def copy(result, source, on_scalar):
+            if on_scalar:
+                nc.scalar.copy(result, source)
+            else:
+                nc.vector.tensor_copy(result, source)
+
+        def interleave(grouped_words, turned, on_scalar):
+            copy(grouped_words.rearrange("p (c u) -> p c u", u=2), turned[:].rearrange("p u c -> p c u"), on_scalar)
 
         def gather_values(r, on_scalar, where=None):
             picked = place([P, J], BF16, "picked%d" % r, where)
@@ -124,10 +133,13 @@ def tile_attend_pickboth_kernel(tc, qpool_words, qpool_scales, keys_words, keys_
                 nc.vector.tensor_copy(picked[:], val[r][:].indirect(k_list[:]))
             return picked
 
-        def turn_values(r, picked, number, where=None):
-            grouped = place([P, 4 * P], BF16, "v_grouped%d" % r, where)
+        def turn_values(picked, number):
             words = picked[:].bitcast(F32)
-            turn_pairs([words[:, u : 2 * P : 2] for u in range(2)], grouped[:].bitcast(F32), number)
+            return turn_pairs([words[:, u : 2 * P : 2] for u in range(2)], number)
+
+        def group_values(r, turned, on_scalar, where=None):
+            grouped = place([P, 4 * P], BF16, "v_grouped%d" % r, where)
+            interleave(grouped[:].bitcast(F32), turned, on_scalar)
             return grouped
 
         def quantize_values(r, grouped, where=None):
@@ -146,10 +158,7 @@ def tile_attend_pickboth_kernel(tc, qpool_words, qpool_scales, keys_words, keys_
             product = bank([P, width], "product%d_%d" % (r, first), number)
             multiply(product[:], codes[:], scales[:], w_codes[:, columns], w_scales[:, columns])
             result = place([P, width], F32, "result%d_%d" % (r, first), where)
-            if on_scalar:
-                nc.scalar.copy(result[:], product[:])
-            else:
-                nc.vector.tensor_copy(result[:], product[:])
+            copy(result[:], product[:], on_scalar)
             return result[:]
 
         def scatter(r, result, first, last, on_scalar):
@@ -195,7 +204,8 @@ def tile_attend_pickboth_kernel(tc, qpool_words, qpool_scales, keys_words, keys_
             w = place([P, J], BF16, "w%d" % i, where)
             nc.vector.scalar_tensor_tensor(w[:], p[i][:], inverse[i][:], size_rows[:], ALU.mult, ALU.mult)
             words = w[:].bitcast(F32)
-            turn_pairs([words[:, P * u : P * (u + 1)] for u in range(2)], w_grouped[i // 2][:].bitcast(F32)[:, 2 * P * (i % 2) : 2 * P * (i % 2 + 1)], number)
+            turned = turn_pairs([words[:, P * u : P * (u + 1)] for u in range(2)], number)
+            interleave(w_grouped[i // 2][:].bitcast(F32)[:, 2 * P * (i % 2) : 2 * P * (i % 2 + 1)], turned, True)
 
         def quantize_weights(h):
             columns = slice(HALF * h, HALF * (h + 1))
@@ -217,30 +227,31 @@ def tile_attend_pickboth_kernel(tc, qpool_words, qpool_scales, keys_words, keys_
         find_max(3)
         exponentiate(2, 2 * ROW)
         exponentiate(3)
-        grouped0 = turn_values(0, picked0, 6, "s3")
+        grouped0 = group_values(0, turn_values(picked0, 6), True, "s3")
         weigh(0, 4)
-        weigh(1, 5)
-        picked1 = gather_values(1, True, "w1")
+        weigh(1, 5, spare + 512)
+        picked1 = gather_values(1, True, spare + 512)
         invert(2)
         invert(3)
         weigh(2, 7)
         v0 = quantize_values(0, grouped0, spare)
         weigh(3, 0)
         quantize_weights(0)
+        turned1 = turn_values(picked1, 7)
         result00 = product_of(0, v0, 0, 0, 1, True, spare + 512)
-        grouped1 = turn_values(1, picked1, 7)
+        grouped1 = group_values(1, turned1, True)
         scatter(0, result00, 0, 0, True)
         picked2 = gather_values(2, False)
         quantize_weights(1)
         v1 = quantize_values(1, grouped1)
         result01 = product_of(0, v0, 1, 1, 2, True)
-        grouped2 = turn_values(2, picked2, 3, spare)
+        grouped2 = group_values(2, turn_values(picked2, 3), True, spare)
         scatter(0, result01, 1, 1, True)
         picked3 = gather_values(3, False)
         result10 = product_of(1, v1, 0, 0, 4, False, 5 * ROW)
         v2 = quantize_values(2, grouped2, 5 * ROW + 1024)
         scatter(1, result10, 0, 0, False)
-        grouped3 = turn_values(3, picked3, 6)
+        grouped3 = group_values(3, turn_values(picked3, 6), True)
         result11 = product_of(1, v1, 1, 1, 5, True, "picked3")
         v3 = quantize_values(3, grouped3)
         scatter(1, result11, 1, 1, False)

@@ -36,8 +36,8 @@ def tile_attend_pickboth_kernel(tc, qpool_words, qpool_scales, keys_words, keys_
         def bank(shape, name, number):
             return psum.tile(shape, F32, name=name, tag="bank%d" % number)
 
-        def load_words(tile, words):
-            nc.sync.dma_start(tile[:], words[0].rearrange("p c r -> p (c r)").bitcast(I32))
+        def load_words(tile, words, first, last):
+            nc.sync.dma_start(tile[:, first:last], words[0].rearrange("p c r -> p (c r)").bitcast(I32)[:, first:last])
 
         def load_scales(tile, scales, first):
             rows = scales[0].bitcast(I32)
@@ -53,10 +53,12 @@ def tile_attend_pickboth_kernel(tc, qpool_words, qpool_scales, keys_words, keys_
         q_word_pool = place([P, T], I32, "q_word_pool", ROW)
         mask_pair = place([P, 2, J], F32, "mask_pair")
         mask_rows = [mask_pair[:, 0, :], mask_pair[:, 1, :]] + [place([P, J], F32, "mask%d" % i)[:] for i in (2, 3)]
-        val = [place([P, T], F32, "val%d" % r, (2 + r) * ROW) for r in range(4)]
+        val = [place([P, T], F32, "val%d" % r, (3 + r) * ROW) for r in range(4)]
 
         def load_values(r):
-            nc.sync.dma_start(val[r][:], vals[P * r : P * (r + 1), :])
+            width = T if r < 2 else T // 2
+            for c in range(0, T, width):
+                nc.sync.dma_start(val[r][:, c : c + width], vals[P * r : P * (r + 1), c : c + width])
 
         def load_mask(i):
             nc.sync.dma_start(mask_rows[i], mask[P * i : P * (i + 1), :])
@@ -64,24 +66,25 @@ def tile_attend_pickboth_kernel(tc, qpool_words, qpool_scales, keys_words, keys_
         nc.gpsimd.memset(k_byte_pool[:].bitcast(I32), 0)
         nc.vector.memset(q_byte_pool[:].bitcast(I32), 0)
         nc.sync.dma_start(k_list[:], offs2)
-        nc.sync.dma_start(q_list[:], offs)
         nc.sync.dma_start(size_cols[:], size[0].rearrange("(n m) -> n m", m=4))
+        load_words(k_word_pool, keys_words, 0, 3 * T // 8)
         load_scales(k_byte_pool, keys_scales, 0)
-        load_words(k_word_pool, keys_words)
+        load_words(k_word_pool, keys_words, 3 * T // 8, T)
+        load_words(q_word_pool, qpool_words, 0, T // 2)
+        nc.sync.dma_start(q_list[:], offs)
         load_scales(q_byte_pool, qpool_scales, 4)
-        load_words(q_word_pool, qpool_words)
+        load_words(q_word_pool, qpool_words, T // 2, T)
         nc.sync.dma_start(mask_pair[:], mask[0 : 2 * P, :].rearrange("(n p) j -> p n j", p=P))
         load_mask(2)
         load_mask(3)
         for r in range(4):
             load_values(r)
 
-        windows = [place([P, T], F32, "window%d" % r) for r in range(4)]
+        windows = [place([P, T], F32, "window%d" % r) for r in range(2)]
         ident = place([P, P], F32, "ident")
         make_identity(nc, ident[:])
-        nc.vector.memset(windows[0][:].bitcast(I32), 0)
-        for r in (1, 2, 3):
-            nc.gpsimd.memset(windows[r][:].bitcast(I32), 0)
+        for window in windows:
+            nc.vector.memset(window[:].bitcast(I32), 0)
 
         size_all = bank([P, 4, P], "size_all", 7)
         for m in range(4):
@@ -109,6 +112,10 @@ def tile_attend_pickboth_kernel(tc, qpool_words, qpool_scales, keys_words, keys_
             nc.vector.tensor_copy(words[:], q_word_pool[:].bitcast(U32).indirect(q_list[:, 8 * i : 8 * (i + 1)]))
             scores.append(bank([P, J], "score%d" % i, i))
             multiply(scores[i][:], words[:], q_bytes[4:P, P * i : P * (i + 1)], k_words[:], k_bytes[:])
+
+        for r in (2, 3):
+            windows.append(place([P, T], F32, "window%d" % r, (2 * r - 3) * ROW // 2))
+            nc.gpsimd.memset(windows[r][:].bitcast(I32), 0)
 
         def turn_pairs(halves, number):
             turned = bank([P, 2, P], "turned", number)
@@ -148,15 +155,15 @@ def tile_attend_pickboth_kernel(tc, qpool_words, qpool_scales, keys_words, keys_
             nc.vector.quantize_mx(out=codes[:].bitcast(FP8X4), scales=scales[:], in_=grouped[:])
             return codes, scales
 
-        w_codes = place([P, I], U32, "w_codes")
-        w_scales = place([P, I], U8, "w_scales")
+        weights = {}
 
         def product_of(r, operand, first, last, number, on_scalar, where=None):
             codes, scales = operand
-            columns = slice(HALF * first, HALF * (last + 1))
             width = HALF * (last + 1 - first)
             product = bank([P, width], "product%d_%d" % (r, first), number)
-            multiply(product[:], codes[:], scales[:], w_codes[:, columns], w_scales[:, columns])
+            for h in range(first, last + 1):
+                w_codes, w_scales = weights[h]
+                multiply(product[:, HALF * (h - first) : HALF * (h - first + 1)], codes[:], scales[:], w_codes[:], w_scales[:])
             result = place([P, width], F32, "result%d_%d" % (r, first), where)
             copy(result[:], product[:], on_scalar)
             return result[:]
@@ -168,17 +175,18 @@ def tile_attend_pickboth_kernel(tc, qpool_words, qpool_scales, keys_words, keys_
             else:
                 nc.vector.tensor_copy(places, result)
             if last == 1:
-                nc.sync.dma_start(out[P * r : P * (r + 1), :], windows[r][:])
+                for c in (0, T // 2):
+                    nc.sync.dma_start(out[P * r : P * (r + 1), c : c + T // 2], windows[r][:, c : c + T // 2])
 
         s = {}
         neg_max = {}
         p = {}
         total = {}
         inverse = {}
-        w_grouped = [place([P, 2 * I], BF16, "w_grouped%d" % h) for h in range(2)]
+        w_grouped = [place([P, 2 * I], BF16, "w_grouped0"), place([P, 2 * I], BF16, "w_grouped1")]
 
-        def add_mask(i):
-            s[i] = place([P, J], F32, "s%d" % i)
+        def add_mask(i, where=None):
+            s[i] = place([P, J], F32, "s%d" % i, where)
             nc.vector.tensor_tensor(s[i][:], scores[i][:], mask_rows[i], ALU.add)
 
         def find_max(i):
@@ -207,11 +215,13 @@ def tile_attend_pickboth_kernel(tc, qpool_words, qpool_scales, keys_words, keys_
             turned = turn_pairs([words[:, P * u : P * (u + 1)] for u in range(2)], number)
             interleave(w_grouped[i // 2][:].bitcast(F32)[:, 2 * P * (i % 2) : 2 * P * (i % 2 + 1)], turned, True)
 
-        def quantize_weights(h):
-            columns = slice(HALF * h, HALF * (h + 1))
-            nc.vector.quantize_mx(out=w_codes[:, columns].bitcast(FP8X4), scales=w_scales[:, columns], in_=w_grouped[h][:])
+        def quantize_weights(h, where=None):
+            codes = place([P, HALF], U32, "w_codes%d" % h, where)
+            scales = place([P, HALF], U8, "w_scales%d" % h)
+            nc.vector.quantize_mx(out=codes[:].bitcast(FP8X4), scales=scales[:], in_=w_grouped[h][:])
+            weights[h] = codes, scales
 
-        spare = 6 * ROW
+        spare = 7 * ROW
         add_mask(0)
         add_mask(1)
         find_max(0)
@@ -225,31 +235,30 @@ def tile_attend_pickboth_kernel(tc, qpool_words, qpool_scales, keys_words, keys_
         find_max(2)
         invert(1)
         find_max(3)
-        exponentiate(2, 2 * ROW)
+        exponentiate(2, 3 * ROW)
         exponentiate(3)
         grouped0 = group_values(0, turn_values(picked0, 6), True, "s3")
         weigh(0, 4)
-        weigh(1, 5, spare + 512)
-        picked1 = gather_values(1, True, spare + 512)
+        weigh(1, 5)
+        picked1 = gather_values(1, True, "w1")
         invert(2)
         invert(3)
         weigh(2, 7)
         v0 = quantize_values(0, grouped0, spare)
         weigh(3, 0)
         quantize_weights(0)
-        turned1 = turn_values(picked1, 7)
         result00 = product_of(0, v0, 0, 0, 1, True, spare + 512)
-        grouped1 = group_values(1, turned1, True)
         scatter(0, result00, 0, 0, True)
+        turned1 = turn_values(picked1, 7)
         picked2 = gather_values(2, False)
-        quantize_weights(1)
-        v1 = quantize_values(1, grouped1)
+        quantize_weights(1, 5 * ROW)
+        v1 = quantize_values(1, group_values(1, turned1, False, 5 * ROW + 1024))
         result01 = product_of(0, v0, 1, 1, 2, True)
         grouped2 = group_values(2, turn_values(picked2, 3), True, spare)
         scatter(0, result01, 1, 1, True)
         picked3 = gather_values(3, False)
-        result10 = product_of(1, v1, 0, 0, 4, False, 5 * ROW)
-        v2 = quantize_values(2, grouped2, 5 * ROW + 1024)
+        result10 = product_of(1, v1, 0, 0, 4, False, 6 * ROW)
+        v2 = quantize_values(2, grouped2, 6 * ROW + 1024)
         scatter(1, result10, 0, 0, False)
         grouped3 = group_values(3, turn_values(picked3, 6), True)
         result11 = product_of(1, v1, 1, 1, 5, True, "picked3")

@@ -80,11 +80,10 @@ def tile_attend_pickboth_kernel(tc, qpool_words, qpool_scales, keys_words, keys_
         for r in range(4):
             load_values(r)
 
-        windows = [place([P, T], F32, "window%d" % r) for r in range(2)]
+        windows = [place([P, T], F32, "window0")]
         ident = place([P, P], F32, "ident")
         make_identity(nc, ident[:])
-        for window in windows:
-            nc.vector.memset(window[:].bitcast(I32), 0)
+        nc.vector.memset(windows[0][:].bitcast(I32), 0)
 
         size_all = bank([P, 4, P], "size_all", 7)
         for m in range(4):
@@ -108,13 +107,13 @@ def tile_attend_pickboth_kernel(tc, qpool_words, qpool_scales, keys_words, keys_
             )
 
         for i in range(4):
-            words = place([P, P], U32, "q_words%d" % i)
+            words = place([P, P], U32, "q_words%d" % i, 8 * ROW + 4 * P * i)
             nc.vector.tensor_copy(words[:], q_word_pool[:].bitcast(U32).indirect(q_list[:, 8 * i : 8 * (i + 1)]))
             scores.append(bank([P, J], "score%d" % i, i))
             multiply(scores[i][:], words[:], q_bytes[4:P, P * i : P * (i + 1)], k_words[:], k_bytes[:])
 
-        for r in (2, 3):
-            windows.append(place([P, T], F32, "window%d" % r, (2 * r - 3) * ROW // 2))
+        for r, where in ((1, ROW // 2), (2, 3 * ROW // 2), (3, 8 * ROW)):
+            windows.append(place([P, T], F32, "window%d" % r, where))
             nc.gpsimd.memset(windows[r][:].bitcast(I32), 0)
 
         def turn_pairs(halves, number):

@@ -156,14 +156,14 @@ def tile_attend_pickboth_kernel(tc, qpool_words, qpool_scales, keys_words, keys_
 
         weights = {}
 
-        def product_of(r, operand, first, last, number, on_scalar, where=None):
-            codes, scales = operand
-            width = HALF * (last + 1 - first)
-            product = bank([P, width], "product%d_%d" % (r, first), number)
-            for h in range(first, last + 1):
-                w_codes, w_scales = weights[h]
-                multiply(product[:, HALF * (h - first) : HALF * (h - first + 1)], codes[:], scales[:], w_codes[:], w_scales[:])
-            result = place([P, width], F32, "result%d_%d" % (r, first), where)
+        def product_of(r, operand, h, number):
+            product = bank([P, HALF], "product%d_%d" % (r, h), number)
+            multiply(product[:], operand[0][:], operand[1][:], weights[h][0][:], weights[h][1][:])
+            return product
+
+        def result_of(r, operand, h, number, on_scalar, where=None):
+            product = product_of(r, operand, h, number)
+            result = place([P, HALF], F32, "result%d_%d" % (r, h), where)
             copy(result[:], product[:], on_scalar)
             return result[:]
 
@@ -246,25 +246,32 @@ def tile_attend_pickboth_kernel(tc, qpool_words, qpool_scales, keys_words, keys_
         v0 = quantize_values(0, grouped0, spare)
         weigh(3, 0)
         quantize_weights(0)
-        result00 = product_of(0, v0, 0, 0, 1, True, spare + 512)
+        result00 = result_of(0, v0, 0, 1, True, spare + 512)
         scatter(0, result00, 0, 0, True)
         turned1 = turn_values(picked1, 7)
         picked2 = gather_values(2, False)
         quantize_weights(1, 5 * ROW)
         v1 = quantize_values(1, group_values(1, turned1, False, 5 * ROW + 1024))
-        result01 = product_of(0, v0, 1, 1, 2, True)
+        result01 = result_of(0, v0, 1, 2, True)
         grouped2 = group_values(2, turn_values(picked2, 3), True, spare)
         scatter(0, result01, 1, 1, True)
         picked3 = gather_values(3, False)
-        result10 = product_of(1, v1, 0, 0, 4, False, 6 * ROW)
+        result10 = result_of(1, v1, 0, 4, False, 6 * ROW)
         v2 = quantize_values(2, grouped2, 6 * ROW + 1024)
         scatter(1, result10, 0, 0, False)
         grouped3 = group_values(3, turn_values(picked3, 6), True)
-        result11 = product_of(1, v1, 1, 1, 5, True, "picked3")
+        third_products = [product_of(2, v2, h, h) for h in range(2)]
+        result11 = result_of(1, v1, 1, 5, True, 6 * ROW + 1024)
+        third_results = [place([P, HALF], F32, "result2_%d" % h) for h in range(2)]
+        copy(third_results[0][:], third_products[0][:], True)
+        scatter(1, result11, 1, 1, True)
         v3 = quantize_values(3, grouped3)
-        scatter(1, result11, 1, 1, False)
-        result20 = product_of(2, v2, 0, 0, 0, True)
-        result21 = product_of(2, v2, 1, 1, 1, True)
-        scatter(2, result20, 0, 0, True)
-        scatter(2, result21, 1, 1, True)
-        scatter(3, product_of(3, v3, 0, 1, 7, False), 0, 1, False)
+        scatter(2, third_results[0][:], 0, 0, False)
+        copy(third_results[1][:], third_products[1][:], True)
+        scatter(2, third_results[1][:], 1, 1, True)
+        last_product = bank([P, I], "last_product", 7)
+        for h in range(2):
+            multiply(last_product[:, HALF * h : HALF * (h + 1)], v3[0][:], v3[1][:], weights[h][0][:], weights[h][1][:])
+        last_result = place([P, I], F32, "last_result")
+        copy(last_result[:], last_product[:], False)
+        scatter(3, last_result[:], 0, 1, False)

@@ -18,7 +18,18 @@ ACT = mybir.ActivationFunctionType
 
 P = 128
 HALF = 256
+Q_SHIFT = 4
+K_FIRST = 3 * T // 8
+Q_FIRST = T // 2
+
 ROW = 4 * T
+KB = 1024
+K_WORDS = 0
+Q_WORDS = ROW
+VALUES = 3 * ROW
+SPARE = 7 * ROW
+Q_PICKED = 8 * ROW
+SIZE_BANK = 7
 
 
 def tile_attend_pickboth_kernel(tc, qpool_words, qpool_scales, keys_words, keys_scales, vals, mask, size, offs, offs2, out):
@@ -49,11 +60,12 @@ def tile_attend_pickboth_kernel(tc, qpool_words, qpool_scales, keys_words, keys_
         k_byte_pool = place([P, T], U8, "k_byte_pool")
         q_byte_pool = place([P, T], U8, "q_byte_pool")
         size_cols = place([P, 4], F32, "size_cols")
-        k_word_pool = place([P, T], I32, "k_word_pool", 0)
-        q_word_pool = place([P, T], I32, "q_word_pool", ROW)
+        k_word_pool = place([P, T], I32, "k_word_pool", K_WORDS)
+        q_word_pool = place([P, T], I32, "q_word_pool", Q_WORDS)
         mask_pair = place([P, 2, J], F32, "mask_pair")
         mask_rows = [mask_pair[:, 0, :], mask_pair[:, 1, :]] + [place([P, J], F32, "mask%d" % i)[:] for i in (2, 3)]
-        val = [place([P, T], F32, "val%d" % r, (3 + r) * ROW) for r in range(4)]
+        value_at = [VALUES + r * ROW for r in range(4)]
+        val = [place([P, T], F32, "val%d" % r, value_at[r]) for r in range(4)]
 
         def load_values(r):
             width = T if r < 2 else T // 2
@@ -66,14 +78,14 @@ def tile_attend_pickboth_kernel(tc, qpool_words, qpool_scales, keys_words, keys_
         nc.gpsimd.memset(k_byte_pool[:].bitcast(I32), 0)
         nc.vector.memset(q_byte_pool[:].bitcast(I32), 0)
         nc.sync.dma_start(k_list[:], offs2)
+        load_words(k_word_pool, keys_words, 0, K_FIRST)
         nc.sync.dma_start(size_cols[:], size[0].rearrange("(n m) -> n m", m=4))
-        load_words(k_word_pool, keys_words, 0, 3 * T // 8)
         load_scales(k_byte_pool, keys_scales, 0)
-        load_words(k_word_pool, keys_words, 3 * T // 8, T)
-        load_words(q_word_pool, qpool_words, 0, T // 2)
+        load_words(k_word_pool, keys_words, K_FIRST, T)
+        load_words(q_word_pool, qpool_words, 0, Q_FIRST)
         nc.sync.dma_start(q_list[:], offs)
-        load_scales(q_byte_pool, qpool_scales, 4)
-        load_words(q_word_pool, qpool_words, T // 2, T)
+        load_scales(q_byte_pool, qpool_scales, Q_SHIFT)
+        load_words(q_word_pool, qpool_words, Q_FIRST, T)
         nc.sync.dma_start(mask_pair[:], mask[0 : 2 * P, :].rearrange("(n p) j -> p n j", p=P))
         load_mask(2)
         load_mask(3)
@@ -85,7 +97,7 @@ def tile_attend_pickboth_kernel(tc, qpool_words, qpool_scales, keys_words, keys_
         make_identity(nc, ident[:])
         nc.vector.memset(windows[0][:].bitcast(I32), 0)
 
-        size_all = bank([P, 4, P], "size_all", 7)
+        size_all = bank([P, 4, P], "size_all", SIZE_BANK)
         for m in range(4):
             nc.tensor.transpose(size_all[:, m, :], size_cols[:, m : m + 1].to_broadcast([P, P]), ident[:])
         size_rows = place([P, J], F32, "size_rows")
@@ -99,20 +111,20 @@ def tile_attend_pickboth_kernel(tc, qpool_words, qpool_scales, keys_words, keys_
         nc.vector.tensor_copy(k_bytes[:], k_byte_pool[:].indirect(k_list[:]))
         nc.vector.tensor_copy(k_words[:], k_word_pool[:].bitcast(U32).indirect(k_list[:]))
         nc.vector.tensor_copy(q_bytes[:], q_byte_pool[:].indirect(q_list[:]))
-        scores = []
 
         def multiply(result, lhs, lhs_scale, rhs, rhs_scale):
             nc.tensor.matmul_mx(
                 out=result, lhsT=lhs.bitcast(FP8X4), lhsT_scale=lhs_scale, rhs=rhs.bitcast(FP8X4), rhs_scale=rhs_scale, start=True, stop=True
             )
 
+        scores = []
         for i in range(4):
-            words = place([P, P], U32, "q_words%d" % i, 8 * ROW + 4 * P * i)
+            words = place([P, P], U32, "q_words%d" % i, Q_PICKED + 4 * P * i)
             nc.vector.tensor_copy(words[:], q_word_pool[:].bitcast(U32).indirect(q_list[:, 8 * i : 8 * (i + 1)]))
             scores.append(bank([P, J], "score%d" % i, i))
-            multiply(scores[i][:], words[:], q_bytes[4:P, P * i : P * (i + 1)], k_words[:], k_bytes[:])
+            multiply(scores[i][:], words[:], q_bytes[Q_SHIFT:P, P * i : P * (i + 1)], k_words[:], k_bytes[:])
 
-        for r, where in ((1, ROW // 2), (2, 3 * ROW // 2), (3, 8 * ROW)):
+        for r, where in ((1, Q_WORDS - ROW // 2), (2, Q_WORDS + ROW // 2), (3, Q_PICKED)):
             windows.append(place([P, T], F32, "window%d" % r, where))
             nc.gpsimd.memset(windows[r][:].bitcast(I32), 0)
 
@@ -182,10 +194,10 @@ def tile_attend_pickboth_kernel(tc, qpool_words, qpool_scales, keys_words, keys_
         p = {}
         total = {}
         inverse = {}
-        w_grouped = [place([P, 2 * I], BF16, "w_grouped0"), place([P, 2 * I], BF16, "w_grouped1")]
+        w_grouped = [place([P, 4 * HALF], BF16, "w_grouped%d" % h) for h in range(2)]
 
-        def add_mask(i, where=None):
-            s[i] = place([P, J], F32, "s%d" % i, where)
+        def add_mask(i):
+            s[i] = place([P, J], F32, "s%d" % i)
             nc.vector.tensor_tensor(s[i][:], scores[i][:], mask_rows[i], ALU.add)
 
         def find_max(i):
@@ -207,8 +219,8 @@ def tile_attend_pickboth_kernel(tc, qpool_words, qpool_scales, keys_words, keys_
             inverse[i] = place([P, 1], F32, "inverse%d" % i)
             nc.vector.reciprocal(inverse[i][:], total[i][:])
 
-        def weigh(i, number, where=None):
-            w = place([P, J], BF16, "w%d" % i, where)
+        def weigh(i, number):
+            w = place([P, J], BF16, "w%d" % i)
             nc.vector.scalar_tensor_tensor(w[:], p[i][:], inverse[i][:], size_rows[:], ALU.mult, ALU.mult)
             words = w[:].bitcast(F32)
             turned = turn_pairs([words[:, P * u : P * (u + 1)] for u in range(2)], number)
@@ -220,7 +232,6 @@ def tile_attend_pickboth_kernel(tc, qpool_words, qpool_scales, keys_words, keys_
             nc.vector.quantize_mx(out=codes[:].bitcast(FP8X4), scales=scales[:], in_=w_grouped[h][:])
             weights[h] = codes, scales
 
-        spare = 7 * ROW
         add_mask(0)
         add_mask(1)
         find_max(0)
@@ -234,7 +245,7 @@ def tile_attend_pickboth_kernel(tc, qpool_words, qpool_scales, keys_words, keys_
         find_max(2)
         invert(1)
         find_max(3)
-        exponentiate(2, 3 * ROW)
+        exponentiate(2, value_at[0])
         exponentiate(3)
         grouped0 = group_values(0, turn_values(picked0, 6), True, "s3")
         weigh(0, 4)
@@ -242,26 +253,28 @@ def tile_attend_pickboth_kernel(tc, qpool_words, qpool_scales, keys_words, keys_
         picked1 = gather_values(1, True, "w1")
         invert(2)
         invert(3)
-        weigh(2, 7)
-        v0 = quantize_values(0, grouped0, spare)
+        weigh(2, SIZE_BANK)
+        v0 = quantize_values(0, grouped0, SPARE)
         weigh(3, 0)
         quantize_weights(0)
-        result00 = result_of(0, v0, 0, 1, True, spare + 512)
+
+        result00 = result_of(0, v0, 0, 1, True, SPARE + KB // 2)
         scatter(0, result00, 0, 0, True)
-        turned1 = turn_values(picked1, 7)
+        turned1 = turn_values(picked1, SIZE_BANK)
         picked2 = gather_values(2, False)
-        quantize_weights(1, 5 * ROW)
-        v1 = quantize_values(1, group_values(1, turned1, False, 5 * ROW + 1024))
+        quantize_weights(1, value_at[2])
+        v1 = quantize_values(1, group_values(1, turned1, False, value_at[2] + KB))
         result01 = result_of(0, v0, 1, 2, True)
-        grouped2 = group_values(2, turn_values(picked2, 3), True, spare)
+        grouped2 = group_values(2, turn_values(picked2, 3), True, SPARE)
         scatter(0, result01, 1, 1, True)
         picked3 = gather_values(3, False)
-        result10 = result_of(1, v1, 0, 4, False, 6 * ROW)
-        v2 = quantize_values(2, grouped2, 6 * ROW + 1024)
+
+        result10 = result_of(1, v1, 0, 4, False, value_at[3])
+        v2 = quantize_values(2, grouped2, value_at[3] + KB)
         scatter(1, result10, 0, 0, False)
         grouped3 = group_values(3, turn_values(picked3, 6), True)
         third_products = [product_of(2, v2, h, h) for h in range(2)]
-        result11 = result_of(1, v1, 1, 5, True, 6 * ROW + 1024)
+        result11 = result_of(1, v1, 1, 5, True, value_at[3] + KB)
         third_results = [place([P, HALF], F32, "result2_%d" % h) for h in range(2)]
         copy(third_results[0][:], third_products[0][:], True)
         scatter(1, result11, 1, 1, True)
@@ -269,7 +282,8 @@ def tile_attend_pickboth_kernel(tc, qpool_words, qpool_scales, keys_words, keys_
         scatter(2, third_results[0][:], 0, 0, False)
         copy(third_results[1][:], third_products[1][:], True)
         scatter(2, third_results[1][:], 1, 1, True)
-        last_product = bank([P, I], "last_product", 7)
+
+        last_product = bank([P, I], "last_product", SIZE_BANK)
         for h in range(2):
             multiply(last_product[:, HALF * h : HALF * (h + 1)], v3[0][:], v3[1][:], weights[h][0][:], weights[h][1][:])
         last_result = place([P, I], F32, "last_result")

@@ -270,18 +270,19 @@ def tile_attend_pickboth_kernel(tc, qpool_words, qpool_scales, keys_words, keys_
         picked3 = gather_values(3, False)
 
         result10 = result_of(1, v1, 0, 4, False, value_at[3])
-        v2 = quantize_values(2, grouped2, value_at[3] + KB)
+        v2 = quantize_values(2, grouped2, value_at[3] + 2 * KB)
         scatter(1, result10, 0, 0, False)
         grouped3 = group_values(3, turn_values(picked3, 6), True)
         third_products = [product_of(2, v2, h, h) for h in range(2)]
-        result11 = result_of(1, v1, 1, 5, True, value_at[3] + KB)
-        third_results = [place([P, HALF], F32, "result2_%d" % h) for h in range(2)]
-        copy(third_results[0][:], third_products[0][:], True)
+        result20 = place([P, HALF], F32, "result2_0")
+        copy(result20[:], third_products[0][:], True)
+        result11 = result_of(1, v1, 1, 5, True, value_at[3] + 5 * KB // 4)
+        result21 = place([P, HALF], F32, "result2_1", value_at[3] + 9 * KB // 4)
+        copy(result21[:], third_products[1][:], True)
         scatter(1, result11, 1, 1, True)
         v3 = quantize_values(3, grouped3)
-        scatter(2, third_results[0][:], 0, 0, False)
-        copy(third_results[1][:], third_products[1][:], True)
-        scatter(2, third_results[1][:], 1, 1, True)
+        scatter(2, result20[:], 0, 0, False)
+        scatter(2, result21[:], 1, 1, True)
 
         last_product = bank([P, I], "last_product", SIZE_BANK)
         for h in range(2):

@@ -19,7 +19,7 @@ ACT = mybir.ActivationFunctionType
 P = 128
 HALF = 256
 Q_SHIFT = 4
-K_FIRST = 3 * T // 8
+K_FIRST = 5 * T // 8
 Q_FIRST = T // 2
 
 ROW = 4 * T

@@ -146,13 +146,16 @@ def tile_attend_pickboth_kernel(tc, qpool_words, qpool_scales, keys_words, keys_
         def gather_values(r, on_scalar, where=None):
             picked = place([P, J], BF16, "picked%d" % r, where)
             if on_scalar:
-                nc.scalar.activation(picked[:], val[r][:].indirect(k_list[:]), ACT.Copy)
+                dealt = picked[:].rearrange("p (u n e) -> p n u e", u=2, e=2)
+                nc.scalar.activation(dealt, val[r][:].indirect(k_list[:]), ACT.Copy)
             else:
                 nc.vector.tensor_copy(picked[:], val[r][:].indirect(k_list[:]))
             return picked
 
-        def turn_values(picked, number):
+        def turn_values(picked, number, dealt=False):
             words = picked[:].bitcast(F32)
+            if dealt:
+                return turn_pairs([words[:, P * u : P * (u + 1)] for u in range(2)], number)
             return turn_pairs([words[:, u : 2 * P : 2] for u in range(2)], number)
 
         def group_values(r, turned, on_scalar, where=None):
@@ -247,7 +250,7 @@ def tile_attend_pickboth_kernel(tc, qpool_words, qpool_scales, keys_words, keys_
         find_max(3)
         exponentiate(2, value_at[0])
         exponentiate(3)
-        grouped0 = group_values(0, turn_values(picked0, 6), True, "s3")
+        grouped0 = group_values(0, turn_values(picked0, 6, True), True, "s3")
         weigh(0, 4)
         weigh(1, 5)
         picked1 = gather_values(1, True, "w1")
@@ -260,7 +263,7 @@ def tile_attend_pickboth_kernel(tc, qpool_words, qpool_scales, keys_words, keys_
 
         result00 = result_of(0, v0, 0, 1, True, SPARE + KB // 2)
         scatter(0, result00, 0, 0, True)
-        turned1 = turn_values(picked1, SIZE_BANK)
+        turned1 = turn_values(picked1, SIZE_BANK, True)
         picked2 = gather_values(2, False)
         quantize_weights(1, value_at[2])
         v1 = quantize_values(1, group_values(1, turned1, False, value_at[2] + KB))

from contextlib import ExitStack

import concourse.mybir as mybir
from concourse.masks import make_identity

D, T, I, J, E = 512, 2048, 512, 512, 512
FLOPS = 2 * D * I * J + 2 * J * E * I

F32 = mybir.dt.float32
BF16 = mybir.dt.bfloat16
I32 = mybir.dt.int32
U32 = mybir.dt.uint32
U16 = mybir.dt.uint16
U8 = mybir.dt.uint8
FP8X4 = mybir.dt.float8_e4m3fn_x4
ALU = mybir.AluOpType
ACT = mybir.ActivationFunctionType

P = 128
HALF = 256
Q_SHIFT = 4
K_FIRST = 5 * T // 8
Q_FIRST = T // 2

ROW = 4 * T
KB = 1024
K_WORDS = 0
Q_WORDS = ROW
VALUES = 3 * ROW
SPARE = 7 * ROW
Q_PICKED = 8 * ROW
SIZE_BANK = 7


def tile_attend_pickboth_kernel(tc, qpool_words, qpool_scales, keys_words, keys_scales, vals, mask, size, offs, offs2, out):
    nc = tc.nc
    with ExitStack() as ctx:
        keep = ctx.enter_context(tc.tile_pool(name="keep", bufs=1))
        psum = ctx.enter_context(tc.psum_pool(name="psum", bufs=1))
        staged = ctx.enter_context(tc.tile_pool(name="staged", bufs=1))

        def place(shape, dtype, name, where=None):
            if isinstance(where, int):
                return staged.tile(shape, dtype, name=name, offset=where, align_bytes=64)
            return keep.tile(shape, dtype, name=name, tag=where or name, align_bytes=64)

        def bank(shape, name, number):
            return psum.tile(shape, F32, name=name, tag="bank%d" % number)

        def load_words(tile, words, first, last):
            nc.sync.dma_start(tile[:, first:last], words[0].rearrange("p c r -> p (c r)").bitcast(I32)[:, first:last])

        def load_scales(tile, scales, first):
            rows = scales[0].bitcast(I32)
            for m in range(4):
                nc.sync.dma_start(tile[first + m : P : 32, :].bitcast(I32), rows[m:16:4, :])

        q_list = keep.tile([P, I // 16], U16, name="q_list")
        k_list = keep.tile([P, J // 16], U16, name="k_list")
        k_byte_pool = place([P, T], U8, "k_byte_pool")
        q_byte_pool = place([P, T], U8, "q_byte_pool")
        size_cols = place([P, 4], F32, "size_cols")
        k_word_pool = place([P, T], I32, "k_word_pool", K_WORDS)
        q_word_pool = place([P, T], I32, "q_word_pool", Q_WORDS)
        mask_pair = place([P, 2, J], F32, "mask_pair")
        mask_rows = [mask_pair[:, 0, :], mask_pair[:, 1, :]] + [place([P, J], F32, "mask%d" % i)[:] for i in (2, 3)]
        value_at = [VALUES + r * ROW for r in range(4)]
        val = [place([P, T], F32, "val%d" % r, value_at[r]) for r in range(4)]

        def load_values(r):
            width = T if r < 2 else T // 2
            for c in range(0, T, width):
                nc.sync.dma_start(val[r][:, c : c + width], vals[P * r : P * (r + 1), c : c + width])

        def load_mask(i):
            nc.sync.dma_start(mask_rows[i], mask[P * i : P * (i + 1), :])

        nc.gpsimd.memset(k_byte_pool[:].bitcast(I32), 0)
        nc.vector.memset(q_byte_pool[:].bitcast(I32), 0)
        nc.sync.dma_start(k_list[:], offs2)
        load_words(k_word_pool, keys_words, 0, K_FIRST)
        nc.sync.dma_start(size_cols[:], size[0].rearrange("(n m) -> n m", m=4))
        load_scales(k_byte_pool, keys_scales, 0)
        load_words(k_word_pool, keys_words, K_FIRST, T)
        load_words(q_word_pool, qpool_words, 0, Q_FIRST)
        nc.sync.dma_start(q_list[:], offs)
        load_scales(q_byte_pool, qpool_scales, Q_SHIFT)
        load_words(q_word_pool, qpool_words, Q_FIRST, T)
        nc.sync.dma_start(mask_pair[:], mask[0 : 2 * P, :].rearrange("(n p) j -> p n j", p=P))
        load_mask(2)
        load_mask(3)
        for r in range(4):
            load_values(r)

        windows = [place([P, T], F32, "window0")]
        ident = place([P, P], F32, "ident")
        make_identity(nc, ident[:])
        nc.vector.memset(windows[0][:].bitcast(I32), 0)

        size_all = bank([P, 4, P], "size_all", SIZE_BANK)
        for m in range(4):
            nc.tensor.transpose(size_all[:, m, :], size_cols[:, m : m + 1].to_broadcast([P, P]), ident[:])
        size_rows = place([P, J], F32, "size_rows")
        nc.scalar.copy(
            size_rows[:].rearrange("p (u n e) -> p u n e", u=2, e=2), size_all[:].rearrange("p (u e) n -> p u n e", e=2)
        )

        k_words = place([P, J], U32, "k_words")
        k_bytes = place([P, J], U8, "k_bytes")
        q_bytes = place([P, I], U8, "q_bytes")
        nc.vector.tensor_copy(k_bytes[:], k_byte_pool[:].indirect(k_list[:]))
        nc.vector.tensor_copy(k_words[:], k_word_pool[:].bitcast(U32).indirect(k_list[:]))
        nc.vector.tensor_copy(q_bytes[:], q_byte_pool[:].indirect(q_list[:]))

        def multiply(result, lhs, lhs_scale, rhs, rhs_scale):
            nc.tensor.matmul_mx(
                out=result, lhsT=lhs.bitcast(FP8X4), lhsT_scale=lhs_scale, rhs=rhs.bitcast(FP8X4), rhs_scale=rhs_scale, start=True, stop=True
            )

        scores = []
        for i in range(4):
            words = place([P, P], U32, "q_words%d" % i, Q_PICKED + 4 * P * i)
            nc.vector.tensor_copy(words[:], q_word_pool[:].bitcast(U32).indirect(q_list[:, 8 * i : 8 * (i + 1)]))
            scores.append(bank([P, J], "score%d" % i, i))
            multiply(scores[i][:], words[:], q_bytes[Q_SHIFT:P, P * i : P * (i + 1)], k_words[:], k_bytes[:])

        for r, where in ((1, Q_WORDS - ROW // 2), (2, Q_WORDS + ROW // 2), (3, Q_PICKED)):
            windows.append(place([P, T], F32, "window%d" % r, where))
            nc.gpsimd.memset(windows[r][:].bitcast(I32), 0)

        def turn_pairs(halves, number):
            turned = bank([P, 2, P], "turned", number)
            for u in range(2):
                nc.tensor.transpose(turned[:, u, :], halves[u], ident[:])
            return turned

        def copy(result, source, on_scalar):
            if on_scalar:
                nc.scalar.copy(result, source)
            else:
                nc.vector.tensor_copy(result, source)

        def interleave(grouped_words, turned, on_scalar):
            copy(grouped_words.rearrange("p (c u) -> p c u", u=2), turned[:].rearrange("p u c -> p c u"), on_scalar)

        def gather_values(r, on_scalar, where=None):
            picked = place([P, J], BF16, "picked%d" % r, where)
            if on_scalar:
                dealt = picked[:].rearrange("p (u n e) -> p n u e", u=2, e=2)
                nc.scalar.activation(dealt, val[r][:].indirect(k_list[:]), ACT.Copy)
            else:
                nc.vector.tensor_copy(picked[:], val[r][:].indirect(k_list[:]))
            return picked

        def turn_values(picked, number, dealt=False):
            words = picked[:].bitcast(F32)
            if dealt:
                return turn_pairs([words[:, P * u : P * (u + 1)] for u in range(2)], number)
            return turn_pairs([words[:, u : 2 * P : 2] for u in range(2)], number)

        def group_values(r, turned, on_scalar, where=None):
            grouped = place([P, 4 * P], BF16, "v_grouped%d" % r, where)
            interleave(grouped[:].bitcast(F32), turned, on_scalar)
            return grouped

        def quantize_values(r, grouped, where=None):
            codes = place([P, P], U32, "v_codes%d" % r, where)
            scales = place([P, P], U8, "v_scales%d" % r)
            nc.vector.quantize_mx(out=codes[:].bitcast(FP8X4), scales=scales[:], in_=grouped[:])
            return codes, scales

        weights = {}

        def product_of(r, operand, h, number):
            product = bank([P, HALF], "product%d_%d" % (r, h), number)
            multiply(product[:], operand[0][:], operand[1][:], weights[h][0][:], weights[h][1][:])
            return product

        def result_of(r, operand, h, number, on_scalar, where=None):
            product = product_of(r, operand, h, number)
            result = place([P, HALF], F32, "result%d_%d" % (r, h), where)
            copy(result[:], product[:], on_scalar)
            return result[:]

        def scatter(r, result, first, last, on_scalar):
            places = windows[r][:].indirect(q_list[:, 16 * first : 16 * (last + 1)])
            if on_scalar:
                nc.scalar.activation(places, result, ACT.Copy)
            else:
                nc.vector.tensor_copy(places, result)
            if last == 1:
                for c in (0, T // 2):
                    nc.sync.dma_start(out[P * r : P * (r + 1), c : c + T // 2], windows[r][:, c : c + T // 2])

        s = {}
        neg_max = {}
        p = {}
        total = {}
        inverse = {}
        w_grouped = [place([P, 4 * HALF], BF16, "w_grouped%d" % h) for h in range(2)]

        def add_mask(i):
            s[i] = place([P, J], F32, "s%d" % i)
            nc.vector.tensor_tensor(s[i][:], scores[i][:], mask_rows[i], ALU.add)

        def find_max(i):
            neg_max[i] = place([P, 1], F32, "neg_max%d" % i)
            nc.vector.tensor_reduce(neg_max[i][:], s[i][:], mybir.AxisListType.X, ALU.max, negate=True)

        def exponentiate(i, where=None):
            total[i] = place([P, 1], F32, "total%d" % i)
            p[i] = place([P, J], F32, "p%d" % i, where)
            nc.scalar.activation(
                p[i][:].rearrange("p (u n e) -> p u n e", u=2, e=2),
                s[i][:].rearrange("p (n u e) -> p u n e", u=2, e=2),
                ACT.Exp,
                bias=neg_max[i][:],
                accum_out=total[i][:],
            )

        def invert(i):
            inverse[i] = place([P, 1], F32, "inverse%d" % i)
            nc.vector.reciprocal(inverse[i][:], total[i][:])

        def weigh(i, number):
            w = place([P, J], BF16, "w%d" % i)
            nc.vector.scalar_tensor_tensor(w[:], p[i][:], inverse[i][:], size_rows[:], ALU.mult, ALU.mult)
            words = w[:].bitcast(F32)
            turned = turn_pairs([words[:, P * u : P * (u + 1)] for u in range(2)], number)
            interleave(w_grouped[i // 2][:].bitcast(F32)[:, 2 * P * (i % 2) : 2 * P * (i % 2 + 1)], turned, True)

        def quantize_weights(h, where=None):
            codes = place([P, HALF], U32, "w_codes%d" % h, where)
            scales = place([P, HALF], U8, "w_scales%d" % h)
            nc.vector.quantize_mx(out=codes[:].bitcast(FP8X4), scales=scales[:], in_=w_grouped[h][:])
            weights[h] = codes, scales

        add_mask(0)
        add_mask(1)
        find_max(0)
        find_max(1)
        exponentiate(0)
        exponentiate(1)
        picked0 = gather_values(0, True)
        add_mask(2)
        add_mask(3)
        invert(0)
        find_max(2)
        invert(1)
        find_max(3)
        exponentiate(2, value_at[0])
        exponentiate(3)
        grouped0 = group_values(0, turn_values(picked0, 6, True), True, "s3")
        weigh(0, 4)
        weigh(1, 5)
        picked1 = gather_values(1, True, "w1")
        invert(2)
        invert(3)
        weigh(2, SIZE_BANK)
        v0 = quantize_values(0, grouped0, SPARE)
        weigh(3, 0)
        quantize_weights(0)

        result00 = result_of(0, v0, 0, 1, True, SPARE + KB // 2)
        scatter(0, result00, 0, 0, True)
        turned1 = turn_values(picked1, SIZE_BANK, True)
        picked2 = gather_values(2, False)
        quantize_weights(1, value_at[2])
        v1 = quantize_values(1, group_values(1, turned1, False, value_at[2] + KB))
        result01 = result_of(0, v0, 1, 2, True)
        grouped2 = group_values(2, turn_values(picked2, 3), True, SPARE)
        scatter(0, result01, 1, 1, True)
        picked3 = gather_values(3, False)

        result10 = result_of(1, v1, 0, 4, False, value_at[3])
        v2 = quantize_values(2, grouped2, value_at[3] + 2 * KB)
        scatter(1, result10, 0, 0, False)
        grouped3 = group_values(3, turn_values(picked3, 6), True)
        third_products = [product_of(2, v2, h, h) for h in range(2)]
        result20 = place([P, HALF], F32, "result2_0")
        copy(result20[:], third_products[0][:], True)
        result11 = result_of(1, v1, 1, 5, True, value_at[3] + 5 * KB // 4)
        result21 = place([P, HALF], F32, "result2_1", value_at[3] + 9 * KB // 4)
        copy(result21[:], third_products[1][:], True)
        scatter(1, result11, 1, 1, True)
        v3 = quantize_values(3, grouped3)
        scatter(2, result20[:], 0, 0, False)
        scatter(2, result21[:], 1, 1, True)

        last_product = bank([P, I], "last_product", SIZE_BANK)
        for h in range(2):
            multiply(last_product[:, HALF * h : HALF * (h + 1)], v3[0][:], v3[1][:], weights[h][0][:], weights[h][1][:])
        last_result = place([P, I], F32, "last_result")
        copy(last_result[:], last_product[:], False)
        scatter(3, last_result[:], 0, 1, False)
